import numpy as np
import ml_dtypes


def mxq(x, axis, fmt="e4m3"):
    dtype, down = {"e4m3": (ml_dtypes.float8_e4m3fn, 7), "e5m2": (ml_dtypes.float8_e5m2, 14)}[fmt]
    v = np.moveaxis(np.asarray(x, np.float32).astype(ml_dtypes.bfloat16).astype(np.float64), axis, -1)
    blocks = v.reshape(v.shape[:-1] + (-1, 32))
    amax = np.abs(blocks).max(-1, keepdims=True)
    byte = np.maximum(np.where(amax > 0, np.frexp(amax)[1] - 1 + 127, 0) - down, 1)
    scale = np.exp2(byte - 127.0)
    codes = (blocks / scale).astype(np.float32).astype(dtype).astype(np.float64)
    return np.moveaxis((codes * scale).reshape(v.shape), -1, axis)


WIDE = False


def mx_kscale(k):
    if not WIDE:
        return np.ones(k)
    levels = np.array([10, -10, 5, -5, 0])
    if k % 512:
        return np.exp2(np.random.permutation(np.resize(levels, k // 32))).repeat(32)
    a = np.empty((k // 512, 16))
    for p in range(k // 512):
        a[p, :8] = np.random.permutation(np.resize(levels, 8))
        for g in range(8):
            far = levels[np.abs(levels - a[p, g]) >= 10]
            a[p, g + 8] = far[np.random.randint(len(far))]
    return np.exp2(a.ravel()).repeat(32)


BF16 = ml_dtypes.bfloat16


def bf(x):
    return np.asarray(x, np.float32).astype(BF16)


def f64(x):
    return np.asarray(x).astype(np.float64)


E2M1 = np.array([0.0, 0.5, 1.0, 1.5, 2.0, 3.0, 4.0, 6.0, -0.0, -0.5, -1.0, -1.5, -2.0, -3.0, -4.0, -6.0])


def pack_weight(w, fmt):
    k, n = w.shape
    w = f64(bf(w)).reshape(k // 32, 32, n)
    amax = np.abs(w).max(1)
    if fmt == "e4m3":
        byte = np.frexp(amax)[1] - 1 + 127 - 7
    else:
        mant, ex = np.frexp(amax / 6.0)
        byte = np.where(mant > 0.5, ex, ex - 1) + 127
    byte = np.clip(np.where(amax > 0, byte, 1), 1, 254)
    scaled = (w * np.exp2(127.0 - byte)[:, None, :]).reshape(k, n).astype(np.float32)
    by_word = np.ascontiguousarray(scaled.reshape(k // 512, 128, 4, n).transpose(0, 1, 3, 2))
    if fmt == "e4m3":
        words = by_word.astype(ml_dtypes.float8_e4m3fn).view(np.uint8)
    else:
        c = by_word.astype(ml_dtypes.float4_e2m1fn).view(np.uint8) & 0xF
        words = c[..., 0::2] | (c[..., 1::2] << 4)
    return np.ascontiguousarray(words), np.ascontiguousarray(byte.astype(np.uint8).reshape(k // 512, 16, n))


def unpack_weight(words, scales, fmt):
    g, p, n, _ = words.shape
    if fmt == "e4m3":
        vals = np.ascontiguousarray(words).view(ml_dtypes.float8_e4m3fn).astype(np.float64)
    else:
        nib = np.empty((g, p, n, 4), np.uint8)
        nib[..., 0::2] = words & 0xF
        nib[..., 1::2] = words >> 4
        vals = E2M1[nib]
    vals = vals * np.repeat(np.exp2(scales.astype(np.float64) - 127.0), 8, axis=1)[..., None]
    return vals.transpose(0, 1, 3, 2).reshape(g * 512, n)
def pack4(w):
    words, scales = pack_weight(w, "e2m1")
    return words.reshape(words.shape[0], 128, -1), scales


def unpack4(words, scales):
    return unpack_weight(words.reshape(words.shape[0], 128, -1, 2), scales, "e2m1")


M, KO, KR, D, V = 512, 512, 1024, 1536, 2048
Z_STD = 0.6
Y_STD = 0.7


def draw0():
    so, sr = mx_kscale(KO), mx_kscale(KR)
    t = mx_kscale(V)
    h_out = 3.0 * np.random.standard_normal((M, KO)) * so
    w_out = np.random.standard_normal((KO, V)) * Z_STD / (3.0 * np.sqrt(KO)) / so[:, None]
    h_rest = np.random.standard_normal((M, KR)) * sr
    w_rest = np.random.standard_normal((KR, V)) * Z_STD / np.sqrt(KR) / sr[:, None]
    w_rest_words, w_rest_scales = pack4(w_rest)
    wt = np.random.standard_normal((V, D)) / np.sqrt(V) / t[:, None]
    wt_words, wt_scales = pack4(wt)
    log_norm = Z_STD ** 2 + 0.2 * np.random.standard_normal(M)
    targets = np.exp(Y_STD * np.random.standard_normal((M, V)) - Y_STD ** 2 / 2)
    vocab_scale = (1 + 0.1 * np.random.standard_normal(V)) * t
    return {"h_out": bf(h_out), "h_rest": bf(h_rest), "w_out": bf(w_out),
            "w_rest_words": w_rest_words, "w_rest_scales": w_rest_scales,
            "log_norm": bf(log_norm), "targets": bf(targets), "vocab_scale": bf(vocab_scale),
            "wt_words": wt_words, "wt_scales": wt_scales}


def core(h_out, h_rest, w_out, w_rest_words, w_rest_scales, log_norm, targets, vocab_scale, wt_words, wt_scales):
    z = ((mxq(f64(h_out), 1, "e4m3") @ mxq(f64(w_out), 0, "e4m3"))
         + (mxq(f64(h_rest), 1, "e4m3") @ unpack4(w_rest_words, w_rest_scales)))
    e = (np.exp(z - f64(log_norm)[:, None]) - f64(targets)) * f64(vocab_scale)
    return mxq(e, 1, "e4m3") @ unpack4(wt_words, wt_scales)


def e4m3fn_bytes(y):
    return np.clip(np.asarray(y, np.float64), -448.0, 448.0).astype(np.float32).astype(ml_dtypes.float8_e4m3fn).view(np.uint8)


def e4m3fn_values(b):
    return np.asarray(b, np.uint8).view(ml_dtypes.float8_e4m3fn).astype(np.float64)


def setup_inputs():
    d = draw0()
    x0 = np.asarray(d['w_out']).astype(np.float64)
    s = (np.max(np.abs(x0), axis=(1,), keepdims=True) / 448.0).astype(np.float32)
    out = {}
    for k, v in d.items():
        if k == 'w_out':
            out['w_out_bytes'] = e4m3fn_bytes(x0 / s.astype(np.float64))
            out['w_out_scale'] = s
        else:
            out[k] = v
    return out


def reference(h_out, h_rest, w_out_bytes, w_out_scale, w_rest_words, w_rest_scales, log_norm, targets, vocab_scale, wt_words, wt_scales):
    return core(h_out, h_rest, e4m3fn_values(w_out_bytes) * w_out_scale.astype(np.float64), w_rest_words, w_rest_scales, log_norm, targets, vocab_scale, wt_words, wt_scales)

@@ -1,0 +1,434 @@
+from contextlib import ExitStack
+
+import concourse.mybir as mybir
+from concourse.masks import make_identity
+
+M, KO, KR, D, V = 512, 512, 1024, 1536, 2048
+FLOPS = 2 * M * (KO + KR) * V + 2 * M * V * D
+
+F32 = mybir.dt.float32
+BF16 = mybir.dt.bfloat16
+I32 = mybir.dt.int32
+U32 = mybir.dt.uint32
+U8 = mybir.dt.uint8
+F8 = mybir.dt.float8_e4m3fn
+FP8X4 = mybir.dt.float8_e4m3fn_x4
+FP4X4 = mybir.dt.float4_e2m1fn_x4
+ALU = mybir.AluOpType
+ACT = mybir.ActivationFunctionType
+
+P = 128
+N = 512
+MT = M // P
+G = V // N
+DT = D // N
+
+
+def tile_cross_entropy_hidden_gradient_s3_kernel(
+    tc, h_out, h_rest, w_out_bytes, w_out_scale, w_rest_words, w_rest_scales,
+    log_norm, targets, vocab_scale, wt_words, wt_scales, out
+):
+    nc = tc.nc
+    with ExitStack() as ctx:
+        keep = ctx.enter_context(tc.tile_pool(name="keep", bufs=1))
+        epool = ctx.enter_context(tc.tile_pool(name="epool", bufs=3))
+        dpool = ctx.enter_context(tc.tile_pool(name="dpool", bufs=2))
+        opool = ctx.enter_context(tc.tile_pool(name="opool", bufs=4))
+        zpool = ctx.enter_context(tc.psum_pool(name="zpool", bufs=3))
+        tpool = ctx.enter_context(tc.psum_pool(name="tpool", bufs=2))
+        cpool = ctx.enter_context(tc.psum_pool(name="cpool", bufs=3))
+        ctx.enter_context(tc.manual_schedule())
+
+        def kt(shape, dtype, name):
+            return keep.tile(shape, dtype, name=name, align_bytes=64)
+
+        wr_planes = kt([P, 2, V], U8, "wr_planes")
+        wt_planes = kt([P, G, D], U8, "wt_planes")
+        aux = kt([P, P], BF16, "aux")
+        dummy = kt([P, 1], F32, "dummy")
+        ident = kt([P, P], F32, "ident")
+        ident_bf = kt([P, P], BF16, "ident_bf")
+        make_identity(nc, ident[:])
+        nc.vector.memset(dummy[:], 0.0)
+        nc.scalar.activation(out=dummy[:], in_=dummy[:], func=ACT.Exp)
+        nc.vector.memset(aux[:], 0.0)
+        nc.vector.memset(wr_planes[:].bitcast(I32), 0)
+        nc.vector.memset(wt_planes[:].bitcast(I32), 0)
+        nc.vector.tensor_copy(out=ident_bf[:], in_=ident[:])
+
+        w_scale = kt([P, 4], F32, "w_scale")
+        w_view = w_out_bytes.rearrange("(p t) n -> p t n", t=4)
+        bytes0 = kt([P, 4, N], U8, "bytes0")
+        bytes1 = kt([P, 4, N], U8, "bytes1")
+        bytes23 = kt([P, 4, 2 * N], U8, "bytes23")
+        byte_views = [bytes0[:], bytes1[:], bytes23[:, :, 0:N], bytes23[:, :, N:2 * N]]
+        wr_view = w_rest_words.rearrange("g p n -> p g n")
+        wr_tiles = [kt([P, 2, V], U8, "wr%d" % i) for i in range(2)]
+        hr_raw = [kt([P, KR], BF16, "hr0"), kt([P, KR], BF16, "hr1")]
+        hr_raw23 = kt([P, 2, KR], BF16, "hr23")
+        ho_raw = [kt([P, 2, KO], BF16, "ho%d" % i) for i in range(2)]
+        tgt = [kt([P, V], BF16, "tgt%d" % i) for i in range(MT)]
+        wt = [kt([P, 2, 2 * D], U8, "wt%d" % i) for i in range(2)]
+
+        def rows(m):
+            return slice(m * P, (m + 1) * P)
+
+        ho_view = h_out.rearrange("(m p) k -> p m k", p=P)
+        wt_view = wt_words.rearrange("g p n -> p g n")
+        nc.sync.dma_start(out=w_scale[:], in_=w_out_scale.rearrange("(p t) o -> p (t o)", t=4))
+        nc.sync.dma_start(out=aux[0:16, :], in_=vocab_scale.rearrange("(r c) -> r c", c=P))
+        nc.sync.dma_start(out=aux[16:20, :], in_=log_norm.rearrange("(r c) -> r c", c=P))
+        nc.sync.dma_start(out=bytes0[:], in_=w_view[:, :, 0:N])
+        nc.sync.dma_start(out=bytes1[:], in_=w_view[:, :, N:2 * N])
+        nc.sync.dma_start(out=hr_raw[0][:], in_=h_rest[rows(0), :])
+        nc.sync.dma_start(out=ho_raw[0][:], in_=ho_view[:, 0:2, :])
+        nc.sync.dma_start(out=hr_raw[1][:], in_=h_rest[rows(1), :])
+        for q in range(4):
+            nc.sync.dma_start(out=wr_planes[32 * q:32 * q + 4].bitcast(I32),
+                              in_=w_rest_scales[:, 4 * q:4 * q + 4, :].bitcast(I32).rearrange("g r n -> r g n"))
+        nc.sync.dma_start(out=wr_tiles[0][:], in_=wr_view[:, :, 0:V])
+        nc.sync.dma_start(out=bytes23[:], in_=w_view[:, :, 2 * N:4 * N])
+        nc.sync.dma_start(out=hr_raw23[:], in_=h_rest.rearrange("(m p) k -> p m k", p=P)[:, 2:4, :])
+        nc.sync.dma_start(out=ho_raw[1][:], in_=ho_view[:, 2:4, :])
+        nc.sync.dma_start(out=wr_tiles[1][:], in_=wr_view[:, :, V:2 * V])
+        nc.sync.dma_start(out=tgt[0][:], in_=targets[rows(0), :])
+        nc.sync.dma_start(out=tgt[1][:], in_=targets[rows(1), :])
+        for q in range(4):
+            nc.sync.dma_start(out=wt_planes[32 * q:32 * q + 4].bitcast(I32),
+                              in_=wt_scales[:, 4 * q:4 * q + 4, :].bitcast(I32).rearrange("g r n -> r g n"))
+        for i in range(2):
+            nc.sync.dma_start(out=wt[i][:], in_=wt_view[:, 2 * i:2 * i + 2, :])
+        nc.sync.dma_start(out=tgt[2][:], in_=targets[rows(2), :])
+        nc.sync.dma_start(out=tgt[3][:], in_=targets[rows(3), :])
+
+        wide = [kt([P, 4, N], BF16, "wide%d" % g) for g in range(G)]
+        w_grp = [kt([P, N, 4], BF16, "wgrp%d" % g) for g in range(G)]
+        w_codes = [kt([P, N], U32, "wcodes%d" % g) for g in range(G)]
+        w_plane = [kt([P, N], U8, "wplane%d" % g) for g in range(G)]
+
+        def widen(g, t, on_scalar):
+            src = byte_views[g][:, t, :].bitcast(F8)
+            if on_scalar:
+                nc.scalar.activation(out=wide[g][:, t, :], in_=src, func=ACT.Copy, scale=w_scale[:, t:t + 1])
+            else:
+                nc.vector.tensor_scalar(out=wide[g][:, t, :], in0=src, scalar1=w_scale[:, t:t + 1], scalar2=None, op0=ALU.mult)
+
+        def interleave(g):
+            nc.vector.tensor_copy(out=w_grp[g][:].rearrange("p (c i) t -> p c t i", i=4),
+                                  in_=wide[g][:].rearrange("p t (c i) -> p c t i", i=4))
+
+        def quant_w(g):
+            nc.vector.quantize_mx(out=w_codes[g][:].bitcast(FP8X4), scales=w_plane[g][:],
+                                  in_=w_grp[g][:].rearrange("p n t -> p (n t)"))
+
+        h_src = {}
+        for m in range(2):
+            h_src["r%d" % m] = [hr_raw[m][:, 0:N].bitcast(F32), hr_raw[m][:, N:2 * N].bitcast(F32)]
+            h_src["r%d" % (m + 2)] = [hr_raw23[:, m, 0:N].bitcast(F32), hr_raw23[:, m, N:2 * N].bitcast(F32)]
+            h_src["o%d" % m] = [ho_raw[m][:, 0, :].bitcast(F32), ho_raw[m][:, 1, :].bitcast(F32)]
+        h_grp, h_codes, h_plane, h_bank = {}, {}, {}, {}
+        for key in h_src:
+            h_grp[key] = kt([P, 2, P, 4], BF16, "hgrp_" + key)
+            h_codes[key] = kt([P, 2, P], U32, "hcodes_" + key)
+            h_plane[key] = kt([P, 2, P], U8, "hplane_" + key)
+
+        def htrans(key):
+            bank = tpool.tile([P, 4, P], F32, name="tb", tag="t")
+            h_bank[key] = bank
+            for j in range(2):
+                for u in range(2):
+                    nc.tensor.transpose(bank[:, 2 * j + u, :], h_src[key][j][:, u:N // 2:2], ident[:])
+
+        def hcopy(key, on_scalar=True):
+            copy = nc.scalar.copy if on_scalar else nc.vector.tensor_copy
+            copy(out=h_grp[key][:].bitcast(F32), in_=h_bank[key][:].rearrange("p (j u) r -> p j r u", u=2))
+
+        def hquant(key):
+            nc.vector.quantize_mx(out=h_codes[key][:].rearrange("p j r -> p (j r)").bitcast(FP8X4),
+                                  scales=h_plane[key][:].rearrange("p j r -> p (j r)"),
+                                  in_=h_grp[key][:].rearrange("p j r t -> p (j r t)"))
+
+        vs = kt([P, V], BF16, "vs")
+        nln = kt([P, MT], F32, "nln")
+        vs_bank = {}
+
+        ln_bank = []
+
+        def ln_trans():
+            bank = tpool.tile([P, P], BF16, name="lnb", tag="t")
+            ln_bank.append(bank)
+            nc.tensor.transpose(bank[:], aux[:], ident_bf[:])
+
+        def ln_neg():
+            nc.vector.tensor_scalar(out=nln[:], in0=ln_bank[0][:, 16:16 + MT], scalar1=-1.0, scalar2=None, op0=ALU.mult)
+
+        def bcast(i):
+            bank = cpool.tile([P, 2 * N], BF16, name="vsb", tag="c")
+            vs_bank[i] = bank
+            for r in range(8):
+                nc.tensor.matmul(bank[:, r * P:(r + 1) * P], lhsT=ident_bf[:, 8 * i + r:8 * i + r + 1].to_broadcast([P, P]),
+                                 rhs=aux[:], start=True, stop=True)
+
+        def vscopy(g):
+            nc.scalar.copy(out=vs[:, g * N:(g + 1) * N].rearrange("q (u p e) -> q u p e", u=2, e=2),
+                           in_=vs_bank[g // 2][:, (g % 2) * N:(g % 2 + 1) * N].rearrange("q (p u e) -> q u p e", u=2, e=2))
+
+        z_bank, e_tile, d_tile, ep_tile = {}, {}, {}, {}
+
+        def mx(bank, lc, lp, rc, rp, start, stop):
+            nc.tensor.matmul_mx(out=bank, lhsT=lc.bitcast(FP8X4), lhsT_scale=lp, rhs=rc, rhs_scale=rp, start=start, stop=stop)
+
+        def zrest(m, g):
+            bank = zpool.tile([P, N], F32, name="zb", tag="z")
+            z_bank[m, g] = bank
+            key = "r%d" % m
+            for j in range(2):
+                c0 = (g % 2) * 2 * N
+                mx(bank[:], h_codes[key][:, j, :], h_plane[key][:, j, :],
+                   wr_tiles[g // 2][:, j, c0:c0 + 2 * N].bitcast(FP4X4), wr_planes[:, j, g * N:(g + 1) * N], j == 0, False)
+
+        def zout(m, g):
+            key = "o%d" % (m // 2)
+            mx(z_bank[m, g][:], h_codes[key][:, m % 2, :], h_plane[key][:, m % 2, :],
+               w_codes[g][:].bitcast(FP8X4), w_plane[g][:], False, True)
+
+        def zexp(m, g):
+            if m not in e_tile:
+                et = epool.tile([P, V], F32, name="et")
+                e_tile[m] = et
+            nc.scalar.activation(out=e_tile[m][:, g * N:(g + 1) * N], in_=z_bank[m, g][:], func=ACT.Exp, bias=nln[:, m:m + 1])
+
+        def sub(m, half):
+            if m not in d_tile:
+                dt_ = dpool.tile([P, V], F32, name="dt_")
+                d_tile[m] = dt_
+            cols = slice(half * 2 * N, (half + 1) * 2 * N)
+            nc.vector.tensor_tensor(out=d_tile[m][:, cols], in0=e_tile[m][:, cols], in1=tgt[m][:, cols], op=ALU.subtract)
+
+        def mul(m, g):
+            if m not in ep_tile:
+                ep = dpool.tile([P, V], BF16, name="ep", align_bytes=64)
+                ep_tile[m] = ep
+            cols = slice(g * N, (g + 1) * N)
+            nc.vector.tensor_tensor(out=ep_tile[m][:, cols].rearrange("q (u p e) -> q u p e", u=2, e=2),
+                                    in0=d_tile[m][:, cols].rearrange("q (p u e) -> q u p e", u=2, e=2),
+                                    in1=vs[:, cols].rearrange("q (u p e) -> q u p e", u=2, e=2), op=ALU.mult)
+
+        e_grp = [kt([P, G, P, 4], BF16, "egrp%d" % m) for m in range(MT)]
+        e_codes = [kt([P, G, P], U32, "ecodes%d" % m) for m in range(MT)]
+        e_plane = [kt([P, G, P], U8, "eplane%d" % m) for m in range(MT)]
+        t_bank = {}
+
+        def etrans(m, half):
+            bank = tpool.tile([P, 4, P], F32, name="tb", tag="t")
+            t_bank[m, half] = bank
+            words = ep_tile[m][:].bitcast(F32)
+            for j in range(4):
+                c0 = (4 * half + j) * P
+                nc.tensor.transpose(bank[:, j, :], words[:, c0:c0 + P], ident[:])
+
+        def ecopy(m, half, on_scalar=True):
+            copy = nc.scalar.copy if on_scalar else nc.vector.tensor_copy
+            copy(out=e_grp[m][:, 2 * half:2 * half + 2].bitcast(F32),
+                           in_=t_bank[m, half][:].rearrange("p (j u) r -> p j r u", u=2))
+
+        def equant(m, g0, g1):
+            nc.vector.quantize_mx(out=e_codes[m][:, g0:g1].rearrange("p g r -> p (g r)").bitcast(FP8X4),
+                                  scales=e_plane[m][:, g0:g1].rearrange("p g r -> p (g r)"),
+                                  in_=e_grp[m][:, g0:g1].rearrange("p g r t -> p (g r t)"))
+
+        c_bank = {}
+
+        def calloc(m, d):
+            bank = cpool.tile([P, N], F32, name="cb", tag="c")
+            c_bank[m, d] = bank
+
+        def cpass(m, d, g0, g1):
+            if g0 == 0:
+                calloc(m, d)
+            for g in range(g0, g1):
+                mx(c_bank[m, d][:], e_codes[m][:, g, :], e_plane[m][:, g, :],
+                   wt[g // 2][:, g % 2, d * 2 * N:(d + 1) * 2 * N].bitcast(FP4X4), wt_planes[:, g, d * N:(d + 1) * N],
+                   g == 0, g == G - 1)
+
+        def cstore(m, d, on_scalar):
+            ot = opool.tile([P, N], F32, name="ot")
+            if on_scalar:
+                nc.scalar.copy(out=ot[:], in_=c_bank[m, d][:])
+            else:
+                nc.vector.tensor_copy(out=ot[:], in_=c_bank[m, d][:])
+            nc.sync.dma_start(out=out[rows(m), d * N:(d + 1) * N], in_=ot[:])
+
+        ln_trans()
+        bcast(1)
+        ln_neg()
+        widen(0, 0, False)
+        widen(0, 2, True)
+        widen(0, 1, False)
+        widen(1, 0, True)
+        widen(0, 3, False)
+        bcast(0)
+        widen(1, 1, False)
+        widen(1, 3, True)
+        interleave(0)
+        htrans("r0")
+        vscopy(0)
+        vscopy(1)
+        vscopy(2)
+        widen(1, 2, False)
+        htrans("o0")
+        hcopy("r0", True)
+        quant_w(0)
+        hcopy("o0", True)
+        hquant("r0")
+        htrans("r1")
+        interleave(1)
+        zrest(0, 0)
+        hcopy("r1", True)
+        vscopy(3)
+        hquant("o0")
+        widen(2, 1, True)
+        hquant("r1")
+        zout(0, 0)
+        widen(2, 0, False)
+        widen(2, 2, True)
+        zrest(1, 0)
+        widen(3, 1, False)
+        widen(3, 2, False)
+        widen(2, 3, True)
+        zout(1, 0)
+        quant_w(1)
+        htrans("r2")
+        widen(3, 0, True)
+        interleave(2)
+        htrans("o1")
+        widen(3, 3, True)
+        zrest(0, 1)
+        hcopy("r2", True)
+        zout(0, 1)
+        interleave(3)
+        zexp(0, 0)
+        htrans("r3")
+        zexp(1, 0)
+        zrest(1, 1)
+        quant_w(2)
+        zexp(0, 1)
+        zout(1, 1)
+        zrest(0, 2)
+        quant_w(3)
+        zexp(1, 1)
+        zout(0, 2)
+        hquant("r2")
+        hcopy("o1", True)
+        zrest(1, 2)
+        sub(0, 0)
+        hcopy("r3", True)
+        zrest(0, 3)
+        zexp(0, 2)
+        zout(1, 2)
+        hquant("o1")
+        zout(0, 3)
+        hquant("r3")
+        zexp(1, 2)
+        zrest(1, 3)
+        mul(0, 0)
+        zexp(0, 3)
+        zrest(2, 0)
+        mul(0, 1)
+        zrest(2, 1)
+        sub(0, 1)
+        zout(1, 3)
+        zout(2, 0)
+        zexp(1, 3)
+        zout(2, 1)
+        sub(1, 0)
+        etrans(0, 0)
+        zexp(2, 0)
+        zrest(2, 2)
+        zexp(2, 1)
+        ecopy(0, 0, False)
+        zrest(2, 3)
+        mul(0, 2)
+        zout(2, 2)
+        zout(2, 3)
+        zexp(2, 2)
+        mul(0, 3)
+        zrest(3, 0)
+        zexp(2, 3)
+        mul(1, 0)
+        zrest(3, 1)
+        mul(1, 1)
+        zrest(3, 2)
+        equant(0, 0, 2)
+        etrans(0, 1)
+        sub(1, 1)
+        etrans(1, 0)
+        ecopy(0, 1, True)
+        zout(3, 0)
+        ecopy(1, 0, True)
+        zout(3, 1)
+        equant(0, 2, 4)
+        zout(3, 2)
+        mul(1, 2)
+        zexp(3, 0)
+        cpass(0, 0, 0, G)
+        sub(2, 0)
+        zexp(3, 1)
+        zrest(3, 3)
+        cstore(0, 0, True)
+        mul(1, 3)
+        cpass(0, 1, 0, G)
+        zexp(3, 2)
+        mul(2, 0)
+        mul(2, 1)
+        etrans(1, 1)
+        cstore(0, 1, True)
+        equant(1, 0, 2)
+        etrans(2, 0)
+        ecopy(1, 1, True)
+        sub(2, 1)
+        cpass(0, 2, 0, G)
+        ecopy(2, 0, True)
+        equant(1, 2, 4)
+        zout(3, 3)
+        cstore(0, 2, True)
+        mul(2, 2)
+        cpass(1, 0, 0, G)
+        mul(2, 3)
+        zexp(3, 3)
+        sub(3, 0)
+        etrans(2, 1)
+        cstore(1, 0, True)
+        cpass(1, 1, 0, G)
+        ecopy(2, 1, True)
+        sub(3, 1)
+        cpass(1, 2, 0, G)
+        cstore(1, 1, True)
+        equant(2, 0, 2)
+        equant(2, 2, 4)
+        mul(3, 0)
+        cpass(2, 0, 0, G)
+        cstore(1, 2, True)
+        mul(3, 1)
+        mul(3, 2)
+        cpass(2, 1, 0, G)
+        cstore(2, 0, True)
+        mul(3, 3)
+        etrans(3, 0)
+        cstore(2, 1, True)
+        etrans(3, 1)
+        ecopy(3, 0, False)
+        cpass(2, 2, 0, G)
+        ecopy(3, 1, True)
+        equant(3, 0, 2)
+        equant(3, 2, 4)
+        cpass(3, 0, 0, 2)
+        cstore(2, 2, False)
+        cpass(3, 1, 0, 2)
+        cpass(3, 2, 0, 2)
+        cpass(3, 0, 2, 4)
+        cpass(3, 1, 2, 4)
+        cstore(3, 0, False)
+        cpass(3, 2, 2, 4)
+        cstore(3, 1, True)
+        cstore(3, 2, False)

@@ -35,8 +35,8 @@ def tile_cross_entropy_hidden_gradient_s3_kernel(
         dpool = ctx.enter_context(tc.tile_pool(name="dpool", bufs=2))
         opool = ctx.enter_context(tc.tile_pool(name="opool", bufs=4))
         zpool = ctx.enter_context(tc.psum_pool(name="zpool", bufs=3))
-        tpool = ctx.enter_context(tc.psum_pool(name="tpool", bufs=2))
-        cpool = ctx.enter_context(tc.psum_pool(name="cpool", bufs=3))
+        tpool = ctx.enter_context(tc.psum_pool(name="tpool", bufs=3))
+        cpool = ctx.enter_context(tc.psum_pool(name="cpool", bufs=2))
         ctx.enter_context(tc.manual_schedule())
 
         def kt(shape, dtype, name):
@@ -48,6 +48,7 @@ def tile_cross_entropy_hidden_gradient_s3_kernel(
         dummy = kt([P, 1], F32, "dummy")
         ident = kt([P, P], F32, "ident")
         ident_bf = kt([P, P], BF16, "ident_bf")
+        w_scale = kt([P, 4], F32, "w_scale")
         make_identity(nc, ident[:])
         nc.vector.memset(dummy[:], 0.0)
         nc.scalar.activation(out=dummy[:], in_=dummy[:], func=ACT.Exp)
@@ -56,7 +57,6 @@ def tile_cross_entropy_hidden_gradient_s3_kernel(
         nc.vector.memset(wt_planes[:].bitcast(I32), 0)
         nc.vector.tensor_copy(out=ident_bf[:], in_=ident[:])
 
-        w_scale = kt([P, 4], F32, "w_scale")
         w_view = w_out_bytes.rearrange("(p t) n -> p t n", t=4)
         bytes0 = kt([P, 4, N], U8, "bytes0")
         bytes1 = kt([P, 4, N], U8, "bytes1")
@@ -76,11 +76,11 @@ def tile_cross_entropy_hidden_gradient_s3_kernel(
         ho_view = h_out.rearrange("(m p) k -> p m k", p=P)
         wt_view = wt_words.rearrange("g p n -> p g n")
         nc.sync.dma_start(out=w_scale[:], in_=w_out_scale.rearrange("(p t) o -> p (t o)", t=4))
-        nc.sync.dma_start(out=aux[0:16, :], in_=vocab_scale.rearrange("(r c) -> r c", c=P))
-        nc.sync.dma_start(out=aux[16:20, :], in_=log_norm.rearrange("(r c) -> r c", c=P))
         nc.sync.dma_start(out=bytes0[:], in_=w_view[:, :, 0:N])
         nc.sync.dma_start(out=bytes1[:], in_=w_view[:, :, N:2 * N])
         nc.sync.dma_start(out=hr_raw[0][:], in_=h_rest[rows(0), :])
+        nc.sync.dma_start(out=aux[0:16, :], in_=vocab_scale.rearrange("(r c) -> r c", c=P))
+        nc.sync.dma_start(out=aux[16:20, :], in_=log_norm.rearrange("(r c) -> r c", c=P))
         nc.sync.dma_start(out=ho_raw[0][:], in_=ho_view[:, 0:2, :])
         nc.sync.dma_start(out=hr_raw[1][:], in_=h_rest[rows(1), :])
         for q in range(4):
@@ -90,14 +90,14 @@ def tile_cross_entropy_hidden_gradient_s3_kernel(
         nc.sync.dma_start(out=bytes23[:], in_=w_view[:, :, 2 * N:4 * N])
         nc.sync.dma_start(out=hr_raw23[:], in_=h_rest.rearrange("(m p) k -> p m k", p=P)[:, 2:4, :])
         nc.sync.dma_start(out=ho_raw[1][:], in_=ho_view[:, 2:4, :])
-        nc.sync.dma_start(out=wr_tiles[1][:], in_=wr_view[:, :, V:2 * V])
         nc.sync.dma_start(out=tgt[0][:], in_=targets[rows(0), :])
+        nc.sync.dma_start(out=wr_tiles[1][:], in_=wr_view[:, :, V:2 * V])
         nc.sync.dma_start(out=tgt[1][:], in_=targets[rows(1), :])
+        for i in range(2):
+            nc.sync.dma_start(out=wt[i][:], in_=wt_view[:, 2 * i:2 * i + 2, :])
         for q in range(4):
             nc.sync.dma_start(out=wt_planes[32 * q:32 * q + 4].bitcast(I32),
                               in_=wt_scales[:, 4 * q:4 * q + 4, :].bitcast(I32).rearrange("g r n -> r g n"))
-        for i in range(2):
-            nc.sync.dma_start(out=wt[i][:], in_=wt_view[:, 2 * i:2 * i + 2, :])
         nc.sync.dma_start(out=tgt[2][:], in_=targets[rows(2), :])
         nc.sync.dma_start(out=tgt[3][:], in_=targets[rows(3), :])
 
@@ -219,18 +219,18 @@ def tile_cross_entropy_hidden_gradient_s3_kernel(
         e_plane = [kt([P, G, P], U8, "eplane%d" % m) for m in range(MT)]
         t_bank = {}
 
-        def etrans(m, half):
+        def etrans(m, g0, g1):
             bank = tpool.tile([P, 4, P], F32, name="tb", tag="t")
-            t_bank[m, half] = bank
+            t_bank[m, g0] = bank
             words = ep_tile[m][:].bitcast(F32)
-            for j in range(4):
-                c0 = (4 * half + j) * P
+            for j in range(2 * (g1 - g0)):
+                c0 = (2 * g0 + j) * P
                 nc.tensor.transpose(bank[:, j, :], words[:, c0:c0 + P], ident[:])
 
-        def ecopy(m, half, on_scalar=True):
+        def ecopy(m, g0, g1, on_scalar):
             copy = nc.scalar.copy if on_scalar else nc.vector.tensor_copy
-            copy(out=e_grp[m][:, 2 * half:2 * half + 2].bitcast(F32),
-                           in_=t_bank[m, half][:].rearrange("p (j u) r -> p j r u", u=2))
+            copy(out=e_grp[m][:, g0:g1].bitcast(F32),
+                 in_=t_bank[m, g0][:, 0:2 * (g1 - g0)].rearrange("p (j u) r -> p j r u", u=2))
 
         def equant(m, g0, g1):
             nc.vector.quantize_mx(out=e_codes[m][:, g0:g1].rearrange("p g r -> p (g r)").bitcast(FP8X4),
@@ -259,176 +259,176 @@ def tile_cross_entropy_hidden_gradient_s3_kernel(
                 nc.vector.tensor_copy(out=ot[:], in_=c_bank[m, d][:])
             nc.sync.dma_start(out=out[rows(m), d * N:(d + 1) * N], in_=ot[:])
 
+        widen(0, 0, False)
+        widen(0, 1, True)
         ln_trans()
+        widen(0, 2, False)
+        widen(0, 3, True)
         bcast(1)
         ln_neg()
-        widen(0, 0, False)
-        widen(0, 2, True)
-        widen(0, 1, False)
-        widen(1, 0, True)
-        widen(0, 3, False)
-        bcast(0)
         widen(1, 1, False)
-        widen(1, 3, True)
+        widen(1, 2, False)
+        widen(1, 0, True)
         interleave(0)
+        widen(1, 3, True)
+        bcast(0)
+        interleave(1)
         htrans("r0")
         vscopy(0)
         vscopy(1)
-        vscopy(2)
-        widen(1, 2, False)
         htrans("o0")
+        vscopy(2)
         hcopy("r0", True)
         quant_w(0)
+        htrans("r1")
         hcopy("o0", True)
         hquant("r0")
-        htrans("r1")
-        interleave(1)
-        zrest(0, 0)
+        quant_w(1)
         hcopy("r1", True)
-        vscopy(3)
+        zrest(0, 0)
         hquant("o0")
-        widen(2, 1, True)
+        vscopy(3)
         hquant("r1")
         zout(0, 0)
         widen(2, 0, False)
-        widen(2, 2, True)
+        widen(2, 1, True)
+        widen(3, 0, False)
         zrest(1, 0)
+        widen(2, 2, True)
         widen(3, 1, False)
-        widen(3, 2, False)
-        widen(2, 3, True)
         zout(1, 0)
-        quant_w(1)
-        htrans("r2")
-        widen(3, 0, True)
-        interleave(2)
-        htrans("o1")
-        widen(3, 3, True)
+        widen(3, 2, False)
         zrest(0, 1)
-        hcopy("r2", True)
+        widen(2, 3, True)
         zout(0, 1)
-        interleave(3)
+        widen(3, 3, True)
+        interleave(2)
+        htrans("r2")
         zexp(0, 0)
-        htrans("r3")
+        htrans("o1")
         zexp(1, 0)
+        interleave(3)
         zrest(1, 1)
-        quant_w(2)
         zexp(0, 1)
+        htrans("r3")
+        hcopy("r2", True)
+        quant_w(2)
+        hcopy("o1", True)
         zout(1, 1)
+        hquant("r2")
+        hcopy("r3", True)
         zrest(0, 2)
         quant_w(3)
         zexp(1, 1)
-        zout(0, 2)
-        hquant("r2")
-        hcopy("o1", True)
         zrest(1, 2)
+        hquant("o1")
         sub(0, 0)
-        hcopy("r3", True)
+        zout(0, 2)
         zrest(0, 3)
         zexp(0, 2)
         zout(1, 2)
-        hquant("o1")
-        zout(0, 3)
         hquant("r3")
+        zout(0, 3)
         zexp(1, 2)
         zrest(1, 3)
         mul(0, 0)
         zexp(0, 3)
-        zrest(2, 0)
-        mul(0, 1)
-        zrest(2, 1)
-        sub(0, 1)
         zout(1, 3)
-        zout(2, 0)
+        mul(0, 1)
+        zrest(2, 0)
         zexp(1, 3)
-        zout(2, 1)
+        sub(0, 1)
+        etrans(0, 0, 2)
+        zout(2, 0)
+        ecopy(0, 0, 2, True)
         sub(1, 0)
-        etrans(0, 0)
+        zrest(2, 1)
         zexp(2, 0)
         zrest(2, 2)
-        zexp(2, 1)
-        ecopy(0, 0, False)
+        equant(0, 0, 2)
         zrest(2, 3)
         mul(0, 2)
-        zout(2, 2)
-        zout(2, 3)
-        zexp(2, 2)
+        zout(2, 1)
         mul(0, 3)
-        zrest(3, 0)
-        zexp(2, 3)
-        mul(1, 0)
-        zrest(3, 1)
-        mul(1, 1)
-        zrest(3, 2)
-        equant(0, 0, 2)
-        etrans(0, 1)
+        zout(2, 2)
+        zexp(2, 1)
+        zout(2, 3)
         sub(1, 1)
-        etrans(1, 0)
-        ecopy(0, 1, True)
-        zout(3, 0)
-        ecopy(1, 0, True)
-        zout(3, 1)
-        equant(0, 2, 4)
-        zout(3, 2)
-        mul(1, 2)
-        zexp(3, 0)
-        cpass(0, 0, 0, G)
+        etrans(0, 2, 4)
+        zexp(2, 2)
+        zrest(3, 0)
+        ecopy(0, 2, 4, True)
         sub(2, 0)
-        zexp(3, 1)
-        zrest(3, 3)
+        zexp(2, 3)
+        zrest(3, 1)
+        zout(3, 0)
+        equant(0, 2, 4)
+        zrest(3, 2)
+        zexp(3, 0)
+        mul(1, 0)
+        cpass(0, 0, 0, G)
+        mul(1, 1)
+        mul(1, 2)
+        zout(3, 1)
         cstore(0, 0, True)
         mul(1, 3)
+        zout(3, 2)
         cpass(0, 1, 0, G)
-        zexp(3, 2)
+        zexp(3, 1)
         mul(2, 0)
+        zexp(3, 2)
         mul(2, 1)
-        etrans(1, 1)
+        etrans(1, 0, 2)
         cstore(0, 1, True)
-        equant(1, 0, 2)
-        etrans(2, 0)
-        ecopy(1, 1, True)
         sub(2, 1)
-        cpass(0, 2, 0, G)
-        ecopy(2, 0, True)
-        equant(1, 2, 4)
-        zout(3, 3)
-        cstore(0, 2, True)
+        etrans(1, 2, 4)
+        ecopy(1, 0, 2, True)
+        etrans(2, 0, 2)
+        zrest(3, 3)
+        ecopy(1, 2, 4, True)
+        equant(1, 0, 2)
         mul(2, 2)
-        cpass(1, 0, 0, G)
+        ecopy(2, 0, 2, True)
+        zout(3, 3)
+        cpass(0, 2, 0, G)
         mul(2, 3)
         zexp(3, 3)
+        equant(1, 2, 4)
         sub(3, 0)
-        etrans(2, 1)
-        cstore(1, 0, True)
-        cpass(1, 1, 0, G)
-        ecopy(2, 1, True)
+        etrans(2, 2, 4)
+        cstore(0, 2, True)
+        cpass(1, 0, 0, G)
+        ecopy(2, 2, 4, True)
         sub(3, 1)
-        cpass(1, 2, 0, G)
-        cstore(1, 1, True)
+        cpass(1, 1, 0, G)
         equant(2, 0, 2)
+        cstore(1, 0, True)
         equant(2, 2, 4)
         mul(3, 0)
-        cpass(2, 0, 0, G)
-        cstore(1, 2, True)
+        cpass(1, 2, 0, G)
+        cstore(1, 1, True)
         mul(3, 1)
         mul(3, 2)
+        cpass(2, 0, 0, G)
+        cstore(1, 2, True)
+        mul(3, 3)
         cpass(2, 1, 0, G)
         cstore(2, 0, True)
-        mul(3, 3)
-        etrans(3, 0)
+        etrans(3, 0, 2)
         cstore(2, 1, True)
-        etrans(3, 1)
-        ecopy(3, 0, False)
+        etrans(3, 2, 4)
+        ecopy(3, 0, 2, False)
         cpass(2, 2, 0, G)
-        ecopy(3, 1, True)
+        ecopy(3, 2, 4, True)
         equant(3, 0, 2)
         equant(3, 2, 4)
         cpass(3, 0, 0, 2)
-        cstore(2, 2, False)
-        cpass(3, 1, 0, 2)
-        cpass(3, 2, 0, 2)
+        cstore(2, 2, True)
         cpass(3, 0, 2, 4)
+        cpass(3, 1, 0, 2)
+        cstore(3, 0, True)
         cpass(3, 1, 2, 4)
-        cstore(3, 0, False)
-        cpass(3, 2, 2, 4)
+        cpass(3, 2, 0, 2)
         cstore(3, 1, True)
-        cstore(3, 2, False)
+        cpass(3, 2, 2, 4)
+        cstore(3, 2, True)

@@ -3,25 +3,29 @@ from contextlib import ExitStack
 import concourse.mybir as mybir
 from concourse.masks import make_identity
 
-M, KO, KR, D, V = 512, 512, 1024, 1536, 2048
-FLOPS = 2 * M * (KO + KR) * V + 2 * M * V * D
+TOKENS, OUT_CH, REST_CH, HIDDEN, VOCAB = 512, 512, 1024, 1536, 2048
+FLOPS = 2 * TOKENS * (OUT_CH + REST_CH) * VOCAB + 2 * TOKENS * VOCAB * HIDDEN
 
 F32 = mybir.dt.float32
 BF16 = mybir.dt.bfloat16
 I32 = mybir.dt.int32
 U32 = mybir.dt.uint32
 U8 = mybir.dt.uint8
-F8 = mybir.dt.float8_e4m3fn
-FP8X4 = mybir.dt.float8_e4m3fn_x4
-FP4X4 = mybir.dt.float4_e2m1fn_x4
-ALU = mybir.AluOpType
-ACT = mybir.ActivationFunctionType
+E4M3FN = mybir.dt.float8_e4m3fn
+E4M3_X4 = mybir.dt.float8_e4m3fn_x4
+E2M1_X4 = mybir.dt.float4_e2m1fn_x4
+MULT = mybir.AluOpType.mult
+SUBTRACT = mybir.AluOpType.subtract
+EXP = mybir.ActivationFunctionType.Exp
+COPY = mybir.ActivationFunctionType.Copy
 
 P = 128
 N = 512
-MT = M // P
-G = V // N
-DT = D // N
+M_TILES = TOKENS // P
+V_GROUPS = VOCAB // N
+D_GROUPS = HIDDEN // N
+VS_ROWS = VOCAB // P
+BANK_ROWS = VS_ROWS // 2
 
 
 def tile_cross_entropy_hidden_gradient_s3_kernel(
@@ -31,404 +35,371 @@ def tile_cross_entropy_hidden_gradient_s3_kernel(
     nc = tc.nc
     with ExitStack() as ctx:
         keep = ctx.enter_context(tc.tile_pool(name="keep", bufs=1))
-        epool = ctx.enter_context(tc.tile_pool(name="epool", bufs=3))
-        dpool = ctx.enter_context(tc.tile_pool(name="dpool", bufs=2))
-        opool = ctx.enter_context(tc.tile_pool(name="opool", bufs=4))
-        zpool = ctx.enter_context(tc.psum_pool(name="zpool", bufs=3))
-        tpool = ctx.enter_context(tc.psum_pool(name="tpool", bufs=3))
-        cpool = ctx.enter_context(tc.psum_pool(name="cpool", bufs=2))
+        e_pool = ctx.enter_context(tc.tile_pool(name="e_pool", bufs=3))
+        diff_pool = ctx.enter_context(tc.tile_pool(name="diff_pool", bufs=2))
+        store_pool = ctx.enter_context(tc.tile_pool(name="store_pool", bufs=6))
+        z_psum = ctx.enter_context(tc.psum_pool(name="z_psum", bufs=3))
+        t_psum = ctx.enter_context(tc.psum_pool(name="t_psum", bufs=3))
+        o_psum = ctx.enter_context(tc.psum_pool(name="o_psum", bufs=2))
         ctx.enter_context(tc.manual_schedule())
 
-        def kt(shape, dtype, name):
+        def kept(shape, dtype, name):
             return keep.tile(shape, dtype, name=name, align_bytes=64)
-
-        wr_planes = kt([P, 2, V], U8, "wr_planes")
-        wt_planes = kt([P, G, D], U8, "wt_planes")
-        aux = kt([P, P], BF16, "aux")
-        dummy = kt([P, 1], F32, "dummy")
-        ident = kt([P, P], F32, "ident")
-        ident_bf = kt([P, P], BF16, "ident_bf")
-        w_scale = kt([P, 4], F32, "w_scale")
-        make_identity(nc, ident[:])
-        nc.vector.memset(dummy[:], 0.0)
-        nc.scalar.activation(out=dummy[:], in_=dummy[:], func=ACT.Exp)
-        nc.vector.memset(aux[:], 0.0)
-        nc.vector.memset(wr_planes[:].bitcast(I32), 0)
-        nc.vector.memset(wt_planes[:].bitcast(I32), 0)
-        nc.vector.tensor_copy(out=ident_bf[:], in_=ident[:])
-
-        w_view = w_out_bytes.rearrange("(p t) n -> p t n", t=4)
-        bytes0 = kt([P, 4, N], U8, "bytes0")
-        bytes1 = kt([P, 4, N], U8, "bytes1")
-        bytes23 = kt([P, 4, 2 * N], U8, "bytes23")
-        byte_views = [bytes0[:], bytes1[:], bytes23[:, :, 0:N], bytes23[:, :, N:2 * N]]
-        wr_view = w_rest_words.rearrange("g p n -> p g n")
-        wr_tiles = [kt([P, 2, V], U8, "wr%d" % i) for i in range(2)]
-        hr_raw = [kt([P, KR], BF16, "hr0"), kt([P, KR], BF16, "hr1")]
-        hr_raw23 = kt([P, 2, KR], BF16, "hr23")
-        ho_raw = [kt([P, 2, KO], BF16, "ho%d" % i) for i in range(2)]
-        tgt = [kt([P, V], BF16, "tgt%d" % i) for i in range(MT)]
-        wt = [kt([P, 2, 2 * D], U8, "wt%d" % i) for i in range(2)]
 
         def rows(m):
             return slice(m * P, (m + 1) * P)
 
-        ho_view = h_out.rearrange("(m p) k -> p m k", p=P)
+        def cols(g):
+            return slice(g * N, (g + 1) * N)
+
+        wr_scale = kept([P, 2, VOCAB], U8, "wr_scale")
+        wt_scale = kept([P, V_GROUPS, HIDDEN], U8, "wt_scale")
+        vectors = kept([P, P], BF16, "vectors")
+        table = kept([P, 1], F32, "table")
+        ident = kept([P, P], F32, "ident")
+        ident_bf = kept([P, P], BF16, "ident_bf")
+        make_identity(nc, ident[:])
+        nc.vector.memset(table[:], 0.0)
+        nc.scalar.activation(out=table[:], in_=table[:], func=EXP)
+        nc.vector.memset(vectors[:], 0.0)
+        nc.vector.memset(wr_scale[:].bitcast(I32), 0)
+        nc.vector.memset(wt_scale[:].bitcast(I32), 0)
+        nc.vector.tensor_copy(out=ident_bf[:], in_=ident[:])
+
+        w_scale = kept([P, 4], F32, "w_scale")
+        bytes0 = kept([P, 4, N], U8, "bytes0")
+        bytes1 = kept([P, 4, N], U8, "bytes1")
+        bytes23 = kept([P, 4, 2 * N], U8, "bytes23")
+        w_bytes = [bytes0[:], bytes1[:], bytes23[:, :, 0:N], bytes23[:, :, N:2 * N]]
+        wr = [kept([P, 2, VOCAB], U8, "wr%d" % i) for i in range(2)]
+        rest0 = kept([P, REST_CH], BF16, "rest0")
+        rest1 = kept([P, REST_CH], BF16, "rest1")
+        rest23 = kept([P, 2, REST_CH], BF16, "rest23")
+        rest = [rest0[:], rest1[:], rest23[:, 0, :], rest23[:, 1, :]]
+        outlier = [kept([P, 2, OUT_CH], BF16, "outlier%d" % i) for i in range(2)]
+        target = [kept([P, VOCAB], BF16, "target%d" % m) for m in range(M_TILES)]
+        wt = [kept([P, 2, 2 * HIDDEN], U8, "wt%d" % i) for i in range(2)]
+
+        w_view = w_out_bytes.rearrange("(p t) v -> p t v", t=4)
+        wr_view = w_rest_words.rearrange("g p n -> p g n")
         wt_view = wt_words.rearrange("g p n -> p g n")
-        nc.sync.dma_start(out=w_scale[:], in_=w_out_scale.rearrange("(p t) o -> p (t o)", t=4))
-        nc.sync.dma_start(out=bytes0[:], in_=w_view[:, :, 0:N])
-        nc.sync.dma_start(out=bytes1[:], in_=w_view[:, :, N:2 * N])
-        nc.sync.dma_start(out=hr_raw[0][:], in_=h_rest[rows(0), :])
-        nc.sync.dma_start(out=aux[0:16, :], in_=vocab_scale.rearrange("(r c) -> r c", c=P))
-        nc.sync.dma_start(out=aux[16:20, :], in_=log_norm.rearrange("(r c) -> r c", c=P))
-        nc.sync.dma_start(out=ho_raw[0][:], in_=ho_view[:, 0:2, :])
-        nc.sync.dma_start(out=hr_raw[1][:], in_=h_rest[rows(1), :])
-        for q in range(4):
-            nc.sync.dma_start(out=wr_planes[32 * q:32 * q + 4].bitcast(I32),
-                              in_=w_rest_scales[:, 4 * q:4 * q + 4, :].bitcast(I32).rearrange("g r n -> r g n"))
-        nc.sync.dma_start(out=wr_tiles[0][:], in_=wr_view[:, :, 0:V])
-        nc.sync.dma_start(out=bytes23[:], in_=w_view[:, :, 2 * N:4 * N])
-        nc.sync.dma_start(out=hr_raw23[:], in_=h_rest.rearrange("(m p) k -> p m k", p=P)[:, 2:4, :])
-        nc.sync.dma_start(out=ho_raw[1][:], in_=ho_view[:, 2:4, :])
-        nc.sync.dma_start(out=tgt[0][:], in_=targets[rows(0), :])
-        nc.sync.dma_start(out=wr_tiles[1][:], in_=wr_view[:, :, V:2 * V])
-        nc.sync.dma_start(out=tgt[1][:], in_=targets[rows(1), :])
+        outlier_view = h_out.rearrange("(m p) k -> p m k", p=P)
+
+        def load(tile, source):
+            nc.sync.dma_start(out=tile, in_=source)
+
+        def load_scales(plane, source):
+            for q in range(4):
+                load(plane[32 * q:32 * q + 4].bitcast(I32),
+                     source[:, 4 * q:4 * q + 4, :].bitcast(I32).rearrange("g r n -> r g n"))
+
+        load(w_scale[:], w_out_scale.rearrange("(p t) o -> p (t o)", t=4))
+        load(bytes0[:], w_view[:, :, 0:N])
+        load(rest0[:], h_rest[rows(0), :])
+        load(bytes1[:], w_view[:, :, N:2 * N])
+        load(vectors[0:VS_ROWS, :], vocab_scale.rearrange("(r c) -> r c", c=P))
+        load(vectors[VS_ROWS:VS_ROWS + M_TILES, :], log_norm.rearrange("(r c) -> r c", c=P))
+        load(outlier[0][:], outlier_view[:, 0:2, :])
+        load(rest1[:], h_rest[rows(1), :])
+        load_scales(wr_scale, w_rest_scales)
+        load(wr[0][:], wr_view[:, :, 0:VOCAB])
+        load(bytes23[:], w_view[:, :, 2 * N:4 * N])
+        load(rest23[:], h_rest.rearrange("(m p) k -> p m k", p=P)[:, 2:4, :])
+        load(outlier[1][:], outlier_view[:, 2:4, :])
+        load(wr[1][:], wr_view[:, :, VOCAB:2 * VOCAB])
+        load(target[0][:], targets[rows(0), :])
+        load(target[1][:], targets[rows(1), :])
         for i in range(2):
-            nc.sync.dma_start(out=wt[i][:], in_=wt_view[:, 2 * i:2 * i + 2, :])
-        for q in range(4):
-            nc.sync.dma_start(out=wt_planes[32 * q:32 * q + 4].bitcast(I32),
-                              in_=wt_scales[:, 4 * q:4 * q + 4, :].bitcast(I32).rearrange("g r n -> r g n"))
-        nc.sync.dma_start(out=tgt[2][:], in_=targets[rows(2), :])
-        nc.sync.dma_start(out=tgt[3][:], in_=targets[rows(3), :])
+            load(wt[i][:], wt_view[:, 2 * i:2 * i + 2, :])
+        load_scales(wt_scale, wt_scales)
+        load(target[2][:], targets[rows(2), :])
+        load(target[3][:], targets[rows(3), :])
 
-        wide = [kt([P, 4, N], BF16, "wide%d" % g) for g in range(G)]
-        w_grp = [kt([P, N, 4], BF16, "wgrp%d" % g) for g in range(G)]
-        w_codes = [kt([P, N], U32, "wcodes%d" % g) for g in range(G)]
-        w_plane = [kt([P, N], U8, "wplane%d" % g) for g in range(G)]
+        wide = [kept([P, 4, N], BF16, "wide%d" % g) for g in range(V_GROUPS)]
+        w_grouped = [kept([P, N, 4], BF16, "w_grouped%d" % g) for g in range(V_GROUPS)]
+        w_codes = [kept([P, N], U32, "w_codes%d" % g) for g in range(V_GROUPS)]
+        w_codes_scale = [kept([P, N], U8, "w_codes_scale%d" % g) for g in range(V_GROUPS)]
 
-        def widen(g, t, on_scalar):
-            src = byte_views[g][:, t, :].bitcast(F8)
-            if on_scalar:
-                nc.scalar.activation(out=wide[g][:, t, :], in_=src, func=ACT.Copy, scale=w_scale[:, t:t + 1])
-            else:
-                nc.vector.tensor_scalar(out=wide[g][:, t, :], in0=src, scalar1=w_scale[:, t:t + 1], scalar2=None, op0=ALU.mult)
+        def widen(g):
+            for t in range(4):
+                source = w_bytes[g][:, t, :].bitcast(E4M3FN)
+                if t % 2 == 0:
+                    nc.vector.tensor_scalar(out=wide[g][:, t, :], in0=source, scalar1=w_scale[:, t:t + 1],
+                                            scalar2=None, op0=MULT)
+                else:
+                    nc.scalar.activation(out=wide[g][:, t, :], in_=source, func=COPY, scale=w_scale[:, t:t + 1])
 
         def interleave(g):
-            nc.vector.tensor_copy(out=w_grp[g][:].rearrange("p (c i) t -> p c t i", i=4),
+            nc.vector.tensor_copy(out=w_grouped[g][:].rearrange("p (c i) t -> p c t i", i=4),
                                   in_=wide[g][:].rearrange("p t (c i) -> p c t i", i=4))
 
-        def quant_w(g):
-            nc.vector.quantize_mx(out=w_codes[g][:].bitcast(FP8X4), scales=w_plane[g][:],
-                                  in_=w_grp[g][:].rearrange("p n t -> p (n t)"))
+        def quantise_w(g):
+            nc.vector.quantize_mx(out=w_codes[g][:].bitcast(E4M3_X4), scales=w_codes_scale[g][:],
+                                  in_=w_grouped[g][:].rearrange("p v t -> p (v t)"))
 
-        h_src = {}
-        for m in range(2):
-            h_src["r%d" % m] = [hr_raw[m][:, 0:N].bitcast(F32), hr_raw[m][:, N:2 * N].bitcast(F32)]
-            h_src["r%d" % (m + 2)] = [hr_raw23[:, m, 0:N].bitcast(F32), hr_raw23[:, m, N:2 * N].bitcast(F32)]
-            h_src["o%d" % m] = [ho_raw[m][:, 0, :].bitcast(F32), ho_raw[m][:, 1, :].bitcast(F32)]
-        h_grp, h_codes, h_plane, h_bank = {}, {}, {}, {}
-        for key in h_src:
-            h_grp[key] = kt([P, 2, P, 4], BF16, "hgrp_" + key)
-            h_codes[key] = kt([P, 2, P], U32, "hcodes_" + key)
-            h_plane[key] = kt([P, 2, P], U8, "hplane_" + key)
+        h_blocks = {}
+        for m in range(M_TILES):
+            h_blocks["rest", m] = [rest[m][:, cols(j)] for j in range(2)]
+        for i in range(2):
+            h_blocks["outlier", i] = [outlier[i][:, j, :] for j in range(2)]
+        h_grouped, h_codes, h_scale, h_bank = {}, {}, {}, {}
+        for kind, i in h_blocks:
+            h_grouped[kind, i] = kept([P, 2, P, 4], BF16, "h_grouped_%s%d" % (kind, i))
+            h_codes[kind, i] = kept([P, 2, P], U32, "h_codes_%s%d" % (kind, i))
+            h_scale[kind, i] = kept([P, 2, P], U8, "h_scale_%s%d" % (kind, i))
 
-        def htrans(key):
-            bank = tpool.tile([P, 4, P], F32, name="tb", tag="t")
-            h_bank[key] = bank
+        def transpose_h(pair):
+            bank = t_psum.tile([P, 4, P], F32, name="t_bank", tag="t")
+            h_bank[pair] = bank
             for j in range(2):
                 for u in range(2):
-                    nc.tensor.transpose(bank[:, 2 * j + u, :], h_src[key][j][:, u:N // 2:2], ident[:])
+                    nc.tensor.transpose(bank[:, 2 * j + u, :], h_blocks[pair][j].bitcast(F32)[:, u:N // 2:2], ident[:])
 
-        def hcopy(key, on_scalar=True):
-            copy = nc.scalar.copy if on_scalar else nc.vector.tensor_copy
-            copy(out=h_grp[key][:].bitcast(F32), in_=h_bank[key][:].rearrange("p (j u) r -> p j r u", u=2))
+        def copy_h(pair):
+            nc.scalar.copy(out=h_grouped[pair][:].bitcast(F32),
+                           in_=h_bank[pair][:].rearrange("p (j u) r -> p j r u", u=2))
 
-        def hquant(key):
-            nc.vector.quantize_mx(out=h_codes[key][:].rearrange("p j r -> p (j r)").bitcast(FP8X4),
-                                  scales=h_plane[key][:].rearrange("p j r -> p (j r)"),
-                                  in_=h_grp[key][:].rearrange("p j r t -> p (j r t)"))
+        def quantise_h(pair):
+            nc.vector.quantize_mx(out=h_codes[pair][:].rearrange("p j r -> p (j r)").bitcast(E4M3_X4),
+                                  scales=h_scale[pair][:].rearrange("p j r -> p (j r)"),
+                                  in_=h_grouped[pair][:].rearrange("p j r t -> p (j r t)"))
 
-        vs = kt([P, V], BF16, "vs")
-        nln = kt([P, MT], F32, "nln")
+        minus_log_norm = kept([P, M_TILES], F32, "minus_log_norm")
+        vs = kept([P, VOCAB], BF16, "vs")
         vs_bank = {}
 
-        ln_bank = []
+        def turn_log_norm():
+            bank = t_psum.tile([P, P], BF16, name="log_norm_bank", tag="t")
+            nc.tensor.transpose(bank[:], vectors[:], ident_bf[:])
+            nc.vector.tensor_scalar(out=minus_log_norm[:], in0=bank[:, VS_ROWS:VS_ROWS + M_TILES],
+                                    scalar1=-1.0, scalar2=None, op0=MULT)
 
-        def ln_trans():
-            bank = tpool.tile([P, P], BF16, name="lnb", tag="t")
-            ln_bank.append(bank)
-            nc.tensor.transpose(bank[:], aux[:], ident_bf[:])
-
-        def ln_neg():
-            nc.vector.tensor_scalar(out=nln[:], in0=ln_bank[0][:, 16:16 + MT], scalar1=-1.0, scalar2=None, op0=ALU.mult)
-
-        def bcast(i):
-            bank = cpool.tile([P, 2 * N], BF16, name="vsb", tag="c")
+        def spread_vs(i):
+            bank = o_psum.tile([P, BANK_ROWS * P], BF16, name="vs_bank", tag="o")
             vs_bank[i] = bank
-            for r in range(8):
-                nc.tensor.matmul(bank[:, r * P:(r + 1) * P], lhsT=ident_bf[:, 8 * i + r:8 * i + r + 1].to_broadcast([P, P]),
-                                 rhs=aux[:], start=True, stop=True)
+            for r in range(BANK_ROWS):
+                row = i * BANK_ROWS + r
+                nc.tensor.matmul(bank[:, rows(r)], lhsT=ident_bf[:, row:row + 1].to_broadcast([P, P]), rhs=vectors[:],
+                                 start=True, stop=True)
 
-        def vscopy(g):
-            nc.scalar.copy(out=vs[:, g * N:(g + 1) * N].rearrange("q (u p e) -> q u p e", u=2, e=2),
-                           in_=vs_bank[g // 2][:, (g % 2) * N:(g % 2 + 1) * N].rearrange("q (p u e) -> q u p e", u=2, e=2))
+        def copy_vs(g):
+            nc.scalar.copy(out=vs[:, cols(g)].rearrange("q (u w e) -> q u w e", u=2, e=2),
+                           in_=vs_bank[g // 2][:, cols(g % 2)].rearrange("q (w u e) -> q u w e", u=2, e=2))
 
-        z_bank, e_tile, d_tile, ep_tile = {}, {}, {}, {}
+        z_bank, e_tile, diff_tile, grad_tile = {}, {}, {}, {}
 
-        def mx(bank, lc, lp, rc, rp, start, stop):
-            nc.tensor.matmul_mx(out=bank, lhsT=lc.bitcast(FP8X4), lhsT_scale=lp, rhs=rc, rhs_scale=rp, start=start, stop=stop)
-
-        def zrest(m, g):
-            bank = zpool.tile([P, N], F32, name="zb", tag="z")
+        def logits(m, g):
+            bank = z_psum.tile([P, N], F32, name="z_bank", tag="z")
             z_bank[m, g] = bank
-            key = "r%d" % m
+            words = slice((g % 2) * 2 * N, (g % 2 + 1) * 2 * N)
             for j in range(2):
-                c0 = (g % 2) * 2 * N
-                mx(bank[:], h_codes[key][:, j, :], h_plane[key][:, j, :],
-                   wr_tiles[g // 2][:, j, c0:c0 + 2 * N].bitcast(FP4X4), wr_planes[:, j, g * N:(g + 1) * N], j == 0, False)
+                nc.tensor.matmul_mx(
+                    out=bank[:],
+                    lhsT=h_codes["rest", m][:, j, :].bitcast(E4M3_X4), lhsT_scale=h_scale["rest", m][:, j, :],
+                    rhs=wr[g // 2][:, j, words].bitcast(E2M1_X4), rhs_scale=wr_scale[:, j, cols(g)],
+                    start=(j == 0), stop=False)
+            pair = ("outlier", m // 2)
+            nc.tensor.matmul_mx(
+                out=bank[:],
+                lhsT=h_codes[pair][:, m % 2, :].bitcast(E4M3_X4), lhsT_scale=h_scale[pair][:, m % 2, :],
+                rhs=w_codes[g][:].bitcast(E4M3_X4), rhs_scale=w_codes_scale[g][:],
+                start=False, stop=True)
 
-        def zout(m, g):
-            key = "o%d" % (m // 2)
-            mx(z_bank[m, g][:], h_codes[key][:, m % 2, :], h_plane[key][:, m % 2, :],
-               w_codes[g][:].bitcast(FP8X4), w_plane[g][:], False, True)
+        def exponential(m, g):
+            if g == 0:
+                e_m = e_pool.tile([P, VOCAB], F32, name="e_m")
+                e_tile[m] = e_m
+            nc.scalar.activation(out=e_tile[m][:, cols(g)], in_=z_bank[m, g][:], func=EXP, bias=minus_log_norm[:, m:m + 1])
 
-        def zexp(m, g):
-            if m not in e_tile:
-                et = epool.tile([P, V], F32, name="et")
-                e_tile[m] = et
-            nc.scalar.activation(out=e_tile[m][:, g * N:(g + 1) * N], in_=z_bank[m, g][:], func=ACT.Exp, bias=nln[:, m:m + 1])
+        def subtract(m, half):
+            if half == 0:
+                diff_m = diff_pool.tile([P, VOCAB], F32, name="diff_m")
+                diff_tile[m] = diff_m
+            two_groups = slice(half * 2 * N, (half + 1) * 2 * N)
+            nc.vector.tensor_tensor(out=diff_tile[m][:, two_groups], in0=e_tile[m][:, two_groups],
+                                    in1=target[m][:, two_groups], op=SUBTRACT)
 
-        def sub(m, half):
-            if m not in d_tile:
-                dt_ = dpool.tile([P, V], F32, name="dt_")
-                d_tile[m] = dt_
-            cols = slice(half * 2 * N, (half + 1) * 2 * N)
-            nc.vector.tensor_tensor(out=d_tile[m][:, cols], in0=e_tile[m][:, cols], in1=tgt[m][:, cols], op=ALU.subtract)
+        def multiply(m, g):
+            if g == 0:
+                grad_m = diff_pool.tile([P, VOCAB], BF16, name="grad_m", align_bytes=64)
+                grad_tile[m] = grad_m
+            nc.vector.tensor_tensor(out=grad_tile[m][:, cols(g)].rearrange("q (u w e) -> q u w e", u=2, e=2),
+                                    in0=diff_tile[m][:, cols(g)].rearrange("q (w u e) -> q u w e", u=2, e=2),
+                                    in1=vs[:, cols(g)].rearrange("q (u w e) -> q u w e", u=2, e=2), op=MULT)
 
-        def mul(m, g):
-            if m not in ep_tile:
-                ep = dpool.tile([P, V], BF16, name="ep", align_bytes=64)
-                ep_tile[m] = ep
-            cols = slice(g * N, (g + 1) * N)
-            nc.vector.tensor_tensor(out=ep_tile[m][:, cols].rearrange("q (u p e) -> q u p e", u=2, e=2),
-                                    in0=d_tile[m][:, cols].rearrange("q (p u e) -> q u p e", u=2, e=2),
-                                    in1=vs[:, cols].rearrange("q (u p e) -> q u p e", u=2, e=2), op=ALU.mult)
+        g_grouped = [kept([P, V_GROUPS, P, 4], BF16, "g_grouped%d" % m) for m in range(M_TILES)]
+        g_codes = [kept([P, V_GROUPS, P], U32, "g_codes%d" % m) for m in range(M_TILES)]
+        g_scale = [kept([P, V_GROUPS, P], U8, "g_scale%d" % m) for m in range(M_TILES)]
+        g_bank = {}
 
-        e_grp = [kt([P, G, P, 4], BF16, "egrp%d" % m) for m in range(MT)]
-        e_codes = [kt([P, G, P], U32, "ecodes%d" % m) for m in range(MT)]
-        e_plane = [kt([P, G, P], U8, "eplane%d" % m) for m in range(MT)]
-        t_bank = {}
+        def transpose_e(m, half):
+            bank = t_psum.tile([P, 4, P], F32, name="t_bank", tag="t")
+            g_bank[m, half] = bank
+            words = grad_tile[m][:].bitcast(F32)
+            for j in range(4):
+                nc.tensor.transpose(bank[:, j, :], words[:, rows(4 * half + j)], ident[:])
 
-        def etrans(m, g0, g1):
-            bank = tpool.tile([P, 4, P], F32, name="tb", tag="t")
-            t_bank[m, g0] = bank
-            words = ep_tile[m][:].bitcast(F32)
-            for j in range(2 * (g1 - g0)):
-                c0 = (2 * g0 + j) * P
-                nc.tensor.transpose(bank[:, j, :], words[:, c0:c0 + P], ident[:])
+        def copy_e(m, half, copy):
+            copy(out=g_grouped[m][:, 2 * half:2 * half + 2].bitcast(F32),
+                 in_=g_bank[m, half][:].rearrange("p (g u) r -> p g r u", u=2))
 
-        def ecopy(m, g0, g1, on_scalar):
-            copy = nc.scalar.copy if on_scalar else nc.vector.tensor_copy
-            copy(out=e_grp[m][:, g0:g1].bitcast(F32),
-                 in_=t_bank[m, g0][:, 0:2 * (g1 - g0)].rearrange("p (j u) r -> p j r u", u=2))
+        def quantise_e(m, half):
+            groups = slice(2 * half, 2 * half + 2)
+            nc.vector.quantize_mx(out=g_codes[m][:, groups].rearrange("p g r -> p (g r)").bitcast(E4M3_X4),
+                                  scales=g_scale[m][:, groups].rearrange("p g r -> p (g r)"),
+                                  in_=g_grouped[m][:, groups].rearrange("p g r t -> p (g r t)"))
 
-        def equant(m, g0, g1):
-            nc.vector.quantize_mx(out=e_codes[m][:, g0:g1].rearrange("p g r -> p (g r)").bitcast(FP8X4),
-                                  scales=e_plane[m][:, g0:g1].rearrange("p g r -> p (g r)"),
-                                  in_=e_grp[m][:, g0:g1].rearrange("p g r t -> p (g r t)"))
+        def quantise_e_whole(m):
+            nc.vector.quantize_mx(out=g_codes[m][:].rearrange("p g r -> p (g r)").bitcast(E4M3_X4),
+                                  scales=g_scale[m][:].rearrange("p g r -> p (g r)"),
+                                  in_=g_grouped[m][:].rearrange("p g r t -> p (g r t)"))
 
-        c_bank = {}
+        o_bank = {}
 
-        def calloc(m, d):
-            bank = cpool.tile([P, N], F32, name="cb", tag="c")
-            c_bank[m, d] = bank
+        def product(m, first, width, passes_of):
+            bank = o_psum.tile([P, N], F32, name="o_bank", tag="o")
+            o_bank[m, first] = bank
+            for c in range(0, width, passes_of):
+                v0 = first + c
+                for g in range(V_GROUPS):
+                    nc.tensor.matmul_mx(
+                        out=bank[:, c:c + passes_of],
+                        lhsT=g_codes[m][:, g, :].bitcast(E4M3_X4), lhsT_scale=g_scale[m][:, g, :],
+                        rhs=wt[g // 2][:, g % 2, 2 * v0:2 * (v0 + passes_of)].bitcast(E2M1_X4),
+                        rhs_scale=wt_scale[:, g, v0:v0 + passes_of],
+                        start=(g == 0), stop=(g == V_GROUPS - 1))
 
-        def cpass(m, d, g0, g1):
-            if g0 == 0:
-                calloc(m, d)
-            for g in range(g0, g1):
-                mx(c_bank[m, d][:], e_codes[m][:, g, :], e_plane[m][:, g, :],
-                   wt[g // 2][:, g % 2, d * 2 * N:(d + 1) * 2 * N].bitcast(FP4X4), wt_planes[:, g, d * N:(d + 1) * N],
-                   g == 0, g == G - 1)
+        def store(m, first, width, copy):
+            result = store_pool.tile([P, N], F32, name="result")
+            copy(out=result[:, 0:width], in_=o_bank[m, first][:, 0:width])
+            nc.sync.dma_start(out=out[rows(m), first:first + width], in_=result[:, 0:width])
 
-        def cstore(m, d, on_scalar):
-            ot = opool.tile([P, N], F32, name="ot")
-            if on_scalar:
-                nc.scalar.copy(out=ot[:], in_=c_bank[m, d][:])
-            else:
-                nc.vector.tensor_copy(out=ot[:], in_=c_bank[m, d][:])
-            nc.sync.dma_start(out=out[rows(m), d * N:(d + 1) * N], in_=ot[:])
+        scalar_copy, vector_copy = nc.scalar.copy, nc.vector.tensor_copy
 
-        widen(0, 0, False)
-        widen(0, 1, True)
-        ln_trans()
-        widen(0, 2, False)
-        widen(0, 3, True)
-        bcast(1)
-        ln_neg()
-        widen(1, 1, False)
-        widen(1, 2, False)
-        widen(1, 0, True)
+        def out_group(m, d, copy=scalar_copy):
+            product(m, d * N, N, N)
+            store(m, d * N, N, copy)
+
+        widen(0)
+        transpose_h(("rest", 0))
+        widen(1)
+        copy_h(("rest", 0))
+        turn_log_norm()
         interleave(0)
-        widen(1, 3, True)
-        bcast(0)
+        quantise_h(("rest", 0))
+        transpose_h(("outlier", 0))
+        copy_h(("outlier", 0))
+        spread_vs(0)
+        transpose_h(("rest", 1))
+        spread_vs(1)
         interleave(1)
-        htrans("r0")
-        vscopy(0)
-        vscopy(1)
-        htrans("o0")
-        vscopy(2)
-        hcopy("r0", True)
-        quant_w(0)
-        htrans("r1")
-        hcopy("o0", True)
-        hquant("r0")
-        quant_w(1)
-        hcopy("r1", True)
-        zrest(0, 0)
-        hquant("o0")
-        vscopy(3)
-        hquant("r1")
-        zout(0, 0)
-        widen(2, 0, False)
-        widen(2, 1, True)
-        widen(3, 0, False)
-        zrest(1, 0)
-        widen(2, 2, True)
-        widen(3, 1, False)
-        zout(1, 0)
-        widen(3, 2, False)
-        zrest(0, 1)
-        widen(2, 3, True)
-        zout(0, 1)
-        widen(3, 3, True)
+        copy_h(("rest", 1))
+        quantise_h(("outlier", 0))
+        quantise_w(0)
+        quantise_h(("rest", 1))
+        quantise_w(1)
+        copy_vs(0)
+        copy_vs(1)
+
+        logits(0, 0)
+        widen(2)
+        logits(1, 0)
+        exponential(0, 0)
+        logits(0, 1)
+        widen(3)
+        exponential(1, 0)
+        exponential(0, 1)
+        logits(1, 1)
         interleave(2)
-        htrans("r2")
-        zexp(0, 0)
-        htrans("o1")
-        zexp(1, 0)
         interleave(3)
-        zrest(1, 1)
-        zexp(0, 1)
-        htrans("r3")
-        hcopy("r2", True)
-        quant_w(2)
-        hcopy("o1", True)
-        zout(1, 1)
-        hquant("r2")
-        hcopy("r3", True)
-        zrest(0, 2)
-        quant_w(3)
-        zexp(1, 1)
-        zrest(1, 2)
-        hquant("o1")
-        sub(0, 0)
-        zout(0, 2)
-        zrest(0, 3)
-        zexp(0, 2)
-        zout(1, 2)
-        hquant("r3")
-        zout(0, 3)
-        zexp(1, 2)
-        zrest(1, 3)
-        mul(0, 0)
-        zexp(0, 3)
-        zout(1, 3)
-        mul(0, 1)
-        zrest(2, 0)
-        zexp(1, 3)
-        sub(0, 1)
-        etrans(0, 0, 2)
-        zout(2, 0)
-        ecopy(0, 0, 2, True)
-        sub(1, 0)
-        zrest(2, 1)
-        zexp(2, 0)
-        zrest(2, 2)
-        equant(0, 0, 2)
-        zrest(2, 3)
-        mul(0, 2)
-        zout(2, 1)
-        mul(0, 3)
-        zout(2, 2)
-        zexp(2, 1)
-        zout(2, 3)
-        sub(1, 1)
-        etrans(0, 2, 4)
-        zexp(2, 2)
-        zrest(3, 0)
-        ecopy(0, 2, 4, True)
-        sub(2, 0)
-        zexp(2, 3)
-        zrest(3, 1)
-        zout(3, 0)
-        equant(0, 2, 4)
-        zrest(3, 2)
-        zexp(3, 0)
-        mul(1, 0)
-        cpass(0, 0, 0, G)
-        mul(1, 1)
-        mul(1, 2)
-        zout(3, 1)
-        cstore(0, 0, True)
-        mul(1, 3)
-        zout(3, 2)
-        cpass(0, 1, 0, G)
-        zexp(3, 1)
-        mul(2, 0)
-        zexp(3, 2)
-        mul(2, 1)
-        etrans(1, 0, 2)
-        cstore(0, 1, True)
-        sub(2, 1)
-        etrans(1, 2, 4)
-        ecopy(1, 0, 2, True)
-        etrans(2, 0, 2)
-        zrest(3, 3)
-        ecopy(1, 2, 4, True)
-        equant(1, 0, 2)
-        mul(2, 2)
-        ecopy(2, 0, 2, True)
-        zout(3, 3)
-        cpass(0, 2, 0, G)
-        mul(2, 3)
-        zexp(3, 3)
-        equant(1, 2, 4)
-        sub(3, 0)
-        etrans(2, 2, 4)
-        cstore(0, 2, True)
-        cpass(1, 0, 0, G)
-        ecopy(2, 2, 4, True)
-        sub(3, 1)
-        cpass(1, 1, 0, G)
-        equant(2, 0, 2)
-        cstore(1, 0, True)
-        equant(2, 2, 4)
-        mul(3, 0)
-        cpass(1, 2, 0, G)
-        cstore(1, 1, True)
-        mul(3, 1)
-        mul(3, 2)
-        cpass(2, 0, 0, G)
-        cstore(1, 2, True)
-        mul(3, 3)
-        cpass(2, 1, 0, G)
-        cstore(2, 0, True)
-        etrans(3, 0, 2)
-        cstore(2, 1, True)
-        etrans(3, 2, 4)
-        ecopy(3, 0, 2, False)
-        cpass(2, 2, 0, G)
-        ecopy(3, 2, 4, True)
-        equant(3, 0, 2)
-        equant(3, 2, 4)
-        cpass(3, 0, 0, 2)
-        cstore(2, 2, True)
-        cpass(3, 0, 2, 4)
-        cpass(3, 1, 0, 2)
-        cstore(3, 0, True)
-        cpass(3, 1, 2, 4)
-        cpass(3, 2, 0, 2)
-        cstore(3, 1, True)
-        cpass(3, 2, 2, 4)
-        cstore(3, 2, True)
+        transpose_h(("rest", 2))
+        copy_h(("rest", 2))
+        exponential(1, 1)
+        transpose_h(("outlier", 1))
+        copy_h(("outlier", 1))
+        transpose_h(("rest", 3))
+        copy_h(("rest", 3))
+        quantise_w(2)
+        subtract(0, 0)
+        quantise_w(3)
+        quantise_h(("rest", 2))
+        multiply(0, 0)
+        multiply(0, 1)
+        quantise_h(("outlier", 1))
+        quantise_h(("rest", 3))
+
+        for g in range(2, 4):
+            for m in range(2):
+                logits(m, g)
+                exponential(m, g)
+        copy_vs(2)
+        copy_vs(3)
+        transpose_e(0, 0)
+        copy_e(0, 0, scalar_copy)
+        subtract(0, 1)
+        quantise_e(0, 0)
+        multiply(0, 2)
+        multiply(0, 3)
+        for g in range(3):
+            logits(2, g)
+            exponential(2, g)
+        transpose_e(0, 1)
+        copy_e(0, 1, scalar_copy)
+        logits(2, 3)
+        exponential(2, 3)
+
+        subtract(1, 0)
+        subtract(1, 1)
+        multiply(1, 0)
+        quantise_e(0, 1)
+        for g in range(1, 4):
+            multiply(1, g)
+        for g in range(3):
+            logits(3, g)
+            exponential(3, g)
+        out_group(0, 0)
+        subtract(2, 0)
+        for half in range(2):
+            transpose_e(1, half)
+        for half in range(2):
+            copy_e(1, half, scalar_copy)
+        out_group(0, 1)
+        subtract(2, 1)
+        logits(3, 3)
+        exponential(3, 3)
+        quantise_e_whole(1)
+        out_group(0, 2)
+
+        for g in range(4):
+            multiply(2, g)
+        subtract(3, 0)
+        out_group(1, 0)
+        for half in range(2):
+            transpose_e(2, half)
+        for half in range(2):
+            copy_e(2, half, scalar_copy)
+        subtract(3, 1)
+        out_group(1, 1)
+        quantise_e_whole(2)
+        out_group(1, 2)
+
+        for g in range(4):
+            multiply(3, g)
+        out_group(2, 0)
+        product(2, N, N, N)
+        for half in range(2):
+            transpose_e(3, half)
+        copy_e(3, 0, vector_copy)
+        copy_e(3, 1, scalar_copy)
+        store(2, N, N, scalar_copy)
+        product(2, 2 * N, N, N)
+        quantise_e(3, 0)
+        quantise_e(3, 1)
+        store(2, 2 * N, N, vector_copy)
+
+        out_group(3, 0)
+        out_group(3, 1)
+        product(3, 2 * N, 3 * P, P)
+        store(3, 2 * N, 3 * P, scalar_copy)
+        product(3, 2 * N + 3 * P, P, P)
+        store(3, 2 * N + 3 * P, P, vector_copy)

@@ -44,7 +44,7 @@ def tile_cross_entropy_hidden_gradient_s3_kernel(
         ctx.enter_context(tc.manual_schedule())
 
         def kept(shape, dtype, name):
-            return keep.tile(shape, dtype, name=name, align_bytes=64)
+            return keep.tile(shape, dtype, name=name, align_bytes=256)
 
         def rows(m):
             return slice(m * P, (m + 1) * P)
@@ -221,7 +221,7 @@ def tile_cross_entropy_hidden_gradient_s3_kernel(
 
         def multiply(m, g):
             if g == 0:
-                grad_m = diff_pool.tile([P, VOCAB], BF16, name="grad_m", align_bytes=64)
+                grad_m = diff_pool.tile([P, VOCAB], BF16, name="grad_m")
                 grad_tile[m] = grad_m
             nc.vector.tensor_tensor(out=grad_tile[m][:, cols(g)].rearrange("q (u w e) -> q u w e", u=2, e=2),
                                     in0=diff_tile[m][:, cols(g)].rearrange("q (w u e) -> q u w e", u=2, e=2),
@@ -289,8 +289,8 @@ def tile_cross_entropy_hidden_gradient_s3_kernel(
         quantise_h(("rest", 0))
         transpose_h(("outlier", 0))
         copy_h(("outlier", 0))
-        spread_vs(0)
         transpose_h(("rest", 1))
+        spread_vs(0)
         spread_vs(1)
         interleave(1)
         copy_h(("rest", 1))
@@ -334,24 +334,23 @@ def tile_cross_entropy_hidden_gradient_s3_kernel(
                 exponential(m, g)
         copy_vs(2)
         copy_vs(3)
-        transpose_e(0, 0)
-        copy_e(0, 0, scalar_copy)
         subtract(0, 1)
-        quantise_e(0, 0)
         multiply(0, 2)
         multiply(0, 3)
         for g in range(3):
             logits(2, g)
             exponential(2, g)
-        transpose_e(0, 1)
-        copy_e(0, 1, scalar_copy)
+        for half in range(2):
+            transpose_e(0, half)
+        for half in range(2):
+            copy_e(0, half, scalar_copy)
         logits(2, 3)
         exponential(2, 3)
 
         subtract(1, 0)
         subtract(1, 1)
         multiply(1, 0)
-        quantise_e(0, 1)
+        quantise_e_whole(0)
         for g in range(1, 4):
             multiply(1, g)
         for g in range(3):

from contextlib import ExitStack

import concourse.mybir as mybir
from concourse.masks import make_identity

TOKENS, OUT_CH, REST_CH, HIDDEN, VOCAB = 512, 512, 1024, 1536, 2048
FLOPS = 2 * TOKENS * (OUT_CH + REST_CH) * VOCAB + 2 * TOKENS * VOCAB * HIDDEN

F32 = mybir.dt.float32
BF16 = mybir.dt.bfloat16
I32 = mybir.dt.int32
U32 = mybir.dt.uint32
U8 = mybir.dt.uint8
E4M3FN = mybir.dt.float8_e4m3fn
E4M3_X4 = mybir.dt.float8_e4m3fn_x4
E2M1_X4 = mybir.dt.float4_e2m1fn_x4
MULT = mybir.AluOpType.mult
SUBTRACT = mybir.AluOpType.subtract
EXP = mybir.ActivationFunctionType.Exp
COPY = mybir.ActivationFunctionType.Copy

P = 128
N = 512
M_TILES = TOKENS // P
V_GROUPS = VOCAB // N
D_GROUPS = HIDDEN // N
VS_ROWS = VOCAB // P
BANK_ROWS = VS_ROWS // 2


def tile_cross_entropy_hidden_gradient_s3_kernel(
    tc, h_out, h_rest, w_out_bytes, w_out_scale, w_rest_words, w_rest_scales,
    log_norm, targets, vocab_scale, wt_words, wt_scales, out
):
    nc = tc.nc
    with ExitStack() as ctx:
        keep = ctx.enter_context(tc.tile_pool(name="keep", bufs=1))
        e_pool = ctx.enter_context(tc.tile_pool(name="e_pool", bufs=3))
        diff_pool = ctx.enter_context(tc.tile_pool(name="diff_pool", bufs=2))
        store_pool = ctx.enter_context(tc.tile_pool(name="store_pool", bufs=6))
        z_psum = ctx.enter_context(tc.psum_pool(name="z_psum", bufs=3))
        t_psum = ctx.enter_context(tc.psum_pool(name="t_psum", bufs=3))
        o_psum = ctx.enter_context(tc.psum_pool(name="o_psum", bufs=2))
        ctx.enter_context(tc.manual_schedule())

        def kept(shape, dtype, name):
            return keep.tile(shape, dtype, name=name, align_bytes=256)

        def rows(m):
            return slice(m * P, (m + 1) * P)

        def cols(g):
            return slice(g * N, (g + 1) * N)

        wr_scale = kept([P, 2, VOCAB], U8, "wr_scale")
        wt_scale = kept([P, V_GROUPS, HIDDEN], U8, "wt_scale")
        vectors = kept([P, P], BF16, "vectors")
        table = kept([P, 1], F32, "table")
        ident = kept([P, P], F32, "ident")
        ident_bf = kept([P, P], BF16, "ident_bf")
        make_identity(nc, ident[:])
        nc.vector.memset(table[:], 0.0)
        nc.scalar.activation(out=table[:], in_=table[:], func=EXP)
        nc.vector.memset(vectors[:], 0.0)
        nc.vector.memset(wr_scale[:].bitcast(I32), 0)
        nc.vector.memset(wt_scale[:].bitcast(I32), 0)
        nc.vector.tensor_copy(out=ident_bf[:], in_=ident[:])

        w_scale = kept([P, 4], F32, "w_scale")
        bytes0 = kept([P, 4, N], U8, "bytes0")
        bytes1 = kept([P, 4, N], U8, "bytes1")
        bytes23 = kept([P, 4, 2 * N], U8, "bytes23")
        w_bytes = [bytes0[:], bytes1[:], bytes23[:, :, 0:N], bytes23[:, :, N:2 * N]]
        wr = [kept([P, 2, VOCAB], U8, "wr%d" % i) for i in range(2)]
        rest0 = kept([P, REST_CH], BF16, "rest0")
        rest1 = kept([P, REST_CH], BF16, "rest1")
        rest23 = kept([P, 2, REST_CH], BF16, "rest23")
        rest = [rest0[:], rest1[:], rest23[:, 0, :], rest23[:, 1, :]]
        outlier = [kept([P, 2, OUT_CH], BF16, "outlier%d" % i) for i in range(2)]
        target = [kept([P, VOCAB], BF16, "target%d" % m) for m in range(M_TILES)]
        wt = [kept([P, 2, 2 * HIDDEN], U8, "wt%d" % i) for i in range(2)]

        w_view = w_out_bytes.rearrange("(p t) v -> p t v", t=4)
        wr_view = w_rest_words.rearrange("g p n -> p g n")
        wt_view = wt_words.rearrange("g p n -> p g n")
        outlier_view = h_out.rearrange("(m p) k -> p m k", p=P)

        def load(tile, source):
            nc.sync.dma_start(out=tile, in_=source)

        def load_scales(plane, source):
            for q in range(4):
                load(plane[32 * q:32 * q + 4].bitcast(I32),
                     source[:, 4 * q:4 * q + 4, :].bitcast(I32).rearrange("g r n -> r g n"))

        load(w_scale[:], w_out_scale.rearrange("(p t) o -> p (t o)", t=4))
        load(bytes0[:], w_view[:, :, 0:N])
        load(rest0[:], h_rest[rows(0), :])
        load(bytes1[:], w_view[:, :, N:2 * N])
        load(vectors[0:VS_ROWS, :], vocab_scale.rearrange("(r c) -> r c", c=P))
        load(vectors[VS_ROWS:VS_ROWS + M_TILES, :], log_norm.rearrange("(r c) -> r c", c=P))
        load(outlier[0][:], outlier_view[:, 0:2, :])
        load(rest1[:], h_rest[rows(1), :])
        load_scales(wr_scale, w_rest_scales)
        load(wr[0][:], wr_view[:, :, 0:VOCAB])
        load(bytes23[:], w_view[:, :, 2 * N:4 * N])
        load(rest23[:], h_rest.rearrange("(m p) k -> p m k", p=P)[:, 2:4, :])
        load(outlier[1][:], outlier_view[:, 2:4, :])
        load(wr[1][:], wr_view[:, :, VOCAB:2 * VOCAB])
        load(target[0][:], targets[rows(0), :])
        load(target[1][:], targets[rows(1), :])
        for i in range(2):
            load(wt[i][:], wt_view[:, 2 * i:2 * i + 2, :])
        load_scales(wt_scale, wt_scales)
        load(target[2][:], targets[rows(2), :])
        load(target[3][:], targets[rows(3), :])

        wide = [kept([P, 4, N], BF16, "wide%d" % g) for g in range(V_GROUPS)]
        w_grouped = [kept([P, N, 4], BF16, "w_grouped%d" % g) for g in range(V_GROUPS)]
        w_codes = [kept([P, N], U32, "w_codes%d" % g) for g in range(V_GROUPS)]
        w_codes_scale = [kept([P, N], U8, "w_codes_scale%d" % g) for g in range(V_GROUPS)]

        def widen(g):
            for t in range(4):
                source = w_bytes[g][:, t, :].bitcast(E4M3FN)
                if t % 2 == 0:
                    nc.vector.tensor_scalar(out=wide[g][:, t, :], in0=source, scalar1=w_scale[:, t:t + 1],
                                            scalar2=None, op0=MULT)
                else:
                    nc.scalar.activation(out=wide[g][:, t, :], in_=source, func=COPY, scale=w_scale[:, t:t + 1])

        def interleave(g):
            nc.vector.tensor_copy(out=w_grouped[g][:].rearrange("p (c i) t -> p c t i", i=4),
                                  in_=wide[g][:].rearrange("p t (c i) -> p c t i", i=4))

        def quantise_w(g):
            nc.vector.quantize_mx(out=w_codes[g][:].bitcast(E4M3_X4), scales=w_codes_scale[g][:],
                                  in_=w_grouped[g][:].rearrange("p v t -> p (v t)"))

        h_blocks = {}
        for m in range(M_TILES):
            h_blocks["rest", m] = [rest[m][:, cols(j)] for j in range(2)]
        for i in range(2):
            h_blocks["outlier", i] = [outlier[i][:, j, :] for j in range(2)]
        h_grouped, h_codes, h_scale, h_bank = {}, {}, {}, {}
        for kind, i in h_blocks:
            h_grouped[kind, i] = kept([P, 2, P, 4], BF16, "h_grouped_%s%d" % (kind, i))
            h_codes[kind, i] = kept([P, 2, P], U32, "h_codes_%s%d" % (kind, i))
            h_scale[kind, i] = kept([P, 2, P], U8, "h_scale_%s%d" % (kind, i))

        def transpose_h(pair):
            bank = t_psum.tile([P, 4, P], F32, name="t_bank", tag="t")
            h_bank[pair] = bank
            for j in range(2):
                for u in range(2):
                    nc.tensor.transpose(bank[:, 2 * j + u, :], h_blocks[pair][j].bitcast(F32)[:, u:N // 2:2], ident[:])

        def copy_h(pair):
            nc.scalar.copy(out=h_grouped[pair][:].bitcast(F32),
                           in_=h_bank[pair][:].rearrange("p (j u) r -> p j r u", u=2))

        def quantise_h(pair):
            nc.vector.quantize_mx(out=h_codes[pair][:].rearrange("p j r -> p (j r)").bitcast(E4M3_X4),
                                  scales=h_scale[pair][:].rearrange("p j r -> p (j r)"),
                                  in_=h_grouped[pair][:].rearrange("p j r t -> p (j r t)"))

        minus_log_norm = kept([P, M_TILES], F32, "minus_log_norm")
        vs = kept([P, VOCAB], BF16, "vs")
        vs_bank = {}

        def turn_log_norm():
            bank = t_psum.tile([P, P], BF16, name="log_norm_bank", tag="t")
            nc.tensor.transpose(bank[:], vectors[:], ident_bf[:])
            nc.vector.tensor_scalar(out=minus_log_norm[:], in0=bank[:, VS_ROWS:VS_ROWS + M_TILES],
                                    scalar1=-1.0, scalar2=None, op0=MULT)

        def spread_vs(i):
            bank = o_psum.tile([P, BANK_ROWS * P], BF16, name="vs_bank", tag="o")
            vs_bank[i] = bank
            for r in range(BANK_ROWS):
                row = i * BANK_ROWS + r
                nc.tensor.matmul(bank[:, rows(r)], lhsT=ident_bf[:, row:row + 1].to_broadcast([P, P]), rhs=vectors[:],
                                 start=True, stop=True)

        def copy_vs(g):
            nc.scalar.copy(out=vs[:, cols(g)].rearrange("q (u w e) -> q u w e", u=2, e=2),
                           in_=vs_bank[g // 2][:, cols(g % 2)].rearrange("q (w u e) -> q u w e", u=2, e=2))

        z_bank, e_tile, diff_tile, grad_tile = {}, {}, {}, {}

        def logits(m, g):
            bank = z_psum.tile([P, N], F32, name="z_bank", tag="z")
            z_bank[m, g] = bank
            words = slice((g % 2) * 2 * N, (g % 2 + 1) * 2 * N)
            for j in range(2):
                nc.tensor.matmul_mx(
                    out=bank[:],
                    lhsT=h_codes["rest", m][:, j, :].bitcast(E4M3_X4), lhsT_scale=h_scale["rest", m][:, j, :],
                    rhs=wr[g // 2][:, j, words].bitcast(E2M1_X4), rhs_scale=wr_scale[:, j, cols(g)],
                    start=(j == 0), stop=False)
            pair = ("outlier", m // 2)
            nc.tensor.matmul_mx(
                out=bank[:],
                lhsT=h_codes[pair][:, m % 2, :].bitcast(E4M3_X4), lhsT_scale=h_scale[pair][:, m % 2, :],
                rhs=w_codes[g][:].bitcast(E4M3_X4), rhs_scale=w_codes_scale[g][:],
                start=False, stop=True)

        def exponential(m, g):
            if g == 0:
                e_m = e_pool.tile([P, VOCAB], F32, name="e_m")
                e_tile[m] = e_m
            nc.scalar.activation(out=e_tile[m][:, cols(g)], in_=z_bank[m, g][:], func=EXP, bias=minus_log_norm[:, m:m + 1])

        def subtract(m, half):
            if half == 0:
                diff_m = diff_pool.tile([P, VOCAB], F32, name="diff_m")
                diff_tile[m] = diff_m
            two_groups = slice(half * 2 * N, (half + 1) * 2 * N)
            nc.vector.tensor_tensor(out=diff_tile[m][:, two_groups], in0=e_tile[m][:, two_groups],
                                    in1=target[m][:, two_groups], op=SUBTRACT)

        def multiply(m, g):
            if g == 0:
                grad_m = diff_pool.tile([P, VOCAB], BF16, name="grad_m")
                grad_tile[m] = grad_m
            nc.vector.tensor_tensor(out=grad_tile[m][:, cols(g)].rearrange("q (u w e) -> q u w e", u=2, e=2),
                                    in0=diff_tile[m][:, cols(g)].rearrange("q (w u e) -> q u w e", u=2, e=2),
                                    in1=vs[:, cols(g)].rearrange("q (u w e) -> q u w e", u=2, e=2), op=MULT)

        g_grouped = [kept([P, V_GROUPS, P, 4], BF16, "g_grouped%d" % m) for m in range(M_TILES)]
        g_codes = [kept([P, V_GROUPS, P], U32, "g_codes%d" % m) for m in range(M_TILES)]
        g_scale = [kept([P, V_GROUPS, P], U8, "g_scale%d" % m) for m in range(M_TILES)]
        g_bank = {}

        def transpose_e(m, half):
            bank = t_psum.tile([P, 4, P], F32, name="t_bank", tag="t")
            g_bank[m, half] = bank
            words = grad_tile[m][:].bitcast(F32)
            for j in range(4):
                nc.tensor.transpose(bank[:, j, :], words[:, rows(4 * half + j)], ident[:])

        def copy_e(m, half, copy):
            copy(out=g_grouped[m][:, 2 * half:2 * half + 2].bitcast(F32),
                 in_=g_bank[m, half][:].rearrange("p (g u) r -> p g r u", u=2))

        def quantise_e(m, half):
            groups = slice(2 * half, 2 * half + 2)
            nc.vector.quantize_mx(out=g_codes[m][:, groups].rearrange("p g r -> p (g r)").bitcast(E4M3_X4),
                                  scales=g_scale[m][:, groups].rearrange("p g r -> p (g r)"),
                                  in_=g_grouped[m][:, groups].rearrange("p g r t -> p (g r t)"))

        def quantise_e_whole(m):
            nc.vector.quantize_mx(out=g_codes[m][:].rearrange("p g r -> p (g r)").bitcast(E4M3_X4),
                                  scales=g_scale[m][:].rearrange("p g r -> p (g r)"),
                                  in_=g_grouped[m][:].rearrange("p g r t -> p (g r t)"))

        o_bank = {}

        def product(m, first, width, passes_of):
            bank = o_psum.tile([P, N], F32, name="o_bank", tag="o")
            o_bank[m, first] = bank
            for c in range(0, width, passes_of):
                v0 = first + c
                for g in range(V_GROUPS):
                    nc.tensor.matmul_mx(
                        out=bank[:, c:c + passes_of],
                        lhsT=g_codes[m][:, g, :].bitcast(E4M3_X4), lhsT_scale=g_scale[m][:, g, :],
                        rhs=wt[g // 2][:, g % 2, 2 * v0:2 * (v0 + passes_of)].bitcast(E2M1_X4),
                        rhs_scale=wt_scale[:, g, v0:v0 + passes_of],
                        start=(g == 0), stop=(g == V_GROUPS - 1))

        def store(m, first, width, copy):
            result = store_pool.tile([P, N], F32, name="result")
            copy(out=result[:, 0:width], in_=o_bank[m, first][:, 0:width])
            nc.sync.dma_start(out=out[rows(m), first:first + width], in_=result[:, 0:width])

        scalar_copy, vector_copy = nc.scalar.copy, nc.vector.tensor_copy

        def out_group(m, d, copy=scalar_copy):
            product(m, d * N, N, N)
            store(m, d * N, N, copy)

        widen(0)
        transpose_h(("rest", 0))
        widen(1)
        copy_h(("rest", 0))
        turn_log_norm()
        interleave(0)
        quantise_h(("rest", 0))
        transpose_h(("outlier", 0))
        copy_h(("outlier", 0))
        transpose_h(("rest", 1))
        spread_vs(0)
        spread_vs(1)
        interleave(1)
        copy_h(("rest", 1))
        quantise_h(("outlier", 0))
        quantise_w(0)
        quantise_h(("rest", 1))
        quantise_w(1)
        copy_vs(0)
        copy_vs(1)

        logits(0, 0)
        widen(2)
        logits(1, 0)
        exponential(0, 0)
        logits(0, 1)
        widen(3)
        exponential(1, 0)
        exponential(0, 1)
        logits(1, 1)
        interleave(2)
        interleave(3)
        transpose_h(("rest", 2))
        copy_h(("rest", 2))
        exponential(1, 1)
        transpose_h(("outlier", 1))
        copy_h(("outlier", 1))
        transpose_h(("rest", 3))
        copy_h(("rest", 3))
        quantise_w(2)
        subtract(0, 0)
        quantise_w(3)
        quantise_h(("rest", 2))
        multiply(0, 0)
        multiply(0, 1)
        quantise_h(("outlier", 1))
        quantise_h(("rest", 3))

        for g in range(2, 4):
            for m in range(2):
                logits(m, g)
                exponential(m, g)
        copy_vs(2)
        copy_vs(3)
        subtract(0, 1)
        multiply(0, 2)
        multiply(0, 3)
        for g in range(3):
            logits(2, g)
            exponential(2, g)
        for half in range(2):
            transpose_e(0, half)
        for half in range(2):
            copy_e(0, half, scalar_copy)
        logits(2, 3)
        exponential(2, 3)

        subtract(1, 0)
        subtract(1, 1)
        multiply(1, 0)
        quantise_e_whole(0)
        for g in range(1, 4):
            multiply(1, g)
        for g in range(3):
            logits(3, g)
            exponential(3, g)
        out_group(0, 0)
        subtract(2, 0)
        for half in range(2):
            transpose_e(1, half)
        for half in range(2):
            copy_e(1, half, scalar_copy)
        out_group(0, 1)
        subtract(2, 1)
        logits(3, 3)
        exponential(3, 3)
        quantise_e_whole(1)
        out_group(0, 2)

        for g in range(4):
            multiply(2, g)
        subtract(3, 0)
        out_group(1, 0)
        for half in range(2):
            transpose_e(2, half)
        for half in range(2):
            copy_e(2, half, scalar_copy)
        subtract(3, 1)
        out_group(1, 1)
        quantise_e_whole(2)
        out_group(1, 2)

        for g in range(4):
            multiply(3, g)
        out_group(2, 0)
        product(2, N, N, N)
        for half in range(2):
            transpose_e(3, half)
        copy_e(3, 0, vector_copy)
        copy_e(3, 1, scalar_copy)
        store(2, N, N, scalar_copy)
        product(2, 2 * N, N, N)
        quantise_e(3, 0)
        quantise_e(3, 1)
        store(2, 2 * N, N, vector_copy)

        out_group(3, 0)
        out_group(3, 1)
        product(3, 2 * N, 3 * P, P)
        store(3, 2 * N, 3 * P, scalar_copy)
        product(3, 2 * N + 3 * P, P, P)
        store(3, 2 * N + 3 * P, P, vector_copy)
